import numpy as np
import ml_dtypes


def mxq(x, axis, fmt="e4m3"):
    dtype, down = {"e4m3": (ml_dtypes.float8_e4m3fn, 7), "e5m2": (ml_dtypes.float8_e5m2, 14)}[fmt]
    v = np.moveaxis(np.asarray(x, np.float32).astype(ml_dtypes.bfloat16).astype(np.float64), axis, -1)
    blocks = v.reshape(v.shape[:-1] + (-1, 32))
    amax = np.abs(blocks).max(-1, keepdims=True)
    byte = np.maximum(np.where(amax > 0, np.frexp(amax)[1] - 1 + 127, 0) - down, 1)
    scale = np.exp2(byte - 127.0)
    codes = (blocks / scale).astype(np.float32).astype(dtype).astype(np.float64)
    return np.moveaxis((codes * scale).reshape(v.shape), -1, axis)


WIDE = False


def mx_kscale(k):
    if not WIDE:
        return np.ones(k)
    levels = np.array([10, -10, 5, -5, 0])
    if k % 512:
        return np.exp2(np.random.permutation(np.resize(levels, k // 32))).repeat(32)
    a = np.empty((k // 512, 16))
    for p in range(k // 512):
        a[p, :8] = np.random.permutation(np.resize(levels, 8))
        for g in range(8):
            far = levels[np.abs(levels - a[p, g]) >= 10]
            a[p, g + 8] = far[np.random.randint(len(far))]
    return np.exp2(a.ravel()).repeat(32)


def f64(x):
    return np.asarray(x).astype(np.float64)


def striped(idx):
    return np.tile(np.asarray(idx).reshape(-1, 16).T, (8, 1)).astype(np.uint16)


def unstriped(offs):
    return offs[:16].T.reshape(-1).astype(np.int64)


G, K, T, D, M = 256, 4, 1024, 1024, 256


def setup_inputs():
    n = np.random.standard_normal
    s = mx_kscale(D)[:, None]
    grid = lambda x: np.round(x * 32) / 32
    x = grid(n((D, T))) * s
    idx = np.random.randint(0, T, (G, K))
    part = np.random.randint(1, 128 // K, (G, K)) / 64.0
    return {
        "xT": x.astype(np.float32),
        "w": (n((D, M)) / np.sqrt(D) / s).astype(np.float32),
        "part": np.tile(part.reshape(-1), (128, 1)).astype(np.float32),
        "bias": (0.3 * n((M, 1))).astype(np.float32),
        "offs": striped(idx.reshape(-1)),
    }


def reference(xT, w, part, bias, offs):
    x = f64(xT)[:, unstriped(offs)]
    y = mxq(f64(w), 0, "e4m3").T @ mxq((x * f64(part)[:1]).reshape(D, G, K).sum(-1), 0, "e4m3")
    y = y + f64(bias)
    return y

@@ -1,0 +1,250 @@
+from contextlib import ExitStack
+
+import concourse.mybir as mybir
+from concourse.masks import make_identity
+
+F32 = mybir.dt.float32
+BF16 = mybir.dt.bfloat16
+U32 = mybir.dt.uint32
+U16 = mybir.dt.uint16
+U8 = mybir.dt.uint8
+FP8X4 = mybir.dt.float8_e4m3fn_x4
+COPY = mybir.ActivationFunctionType.Copy
+IDENTITY = mybir.ActivationFunctionType.Identity
+ADD = mybir.AluOpType.add
+MULT = mybir.AluOpType.mult
+
+P = 128
+D = 1024
+T = 1024
+M = 256
+G = 256
+K = 4
+PACK = 4
+PASSES = D // (P * PACK)
+BLOCKS = G // P
+CHANNELS = M // P
+HALF = T // 2
+ENTRIES = P * K
+LIST_COLUMNS = ENTRIES // 16
+
+FLOPS = 2 * D * M * G
+
+
+def tile_attend_grid_bias_kernel(tc, xT, w, part, bias, offs, out):
+    nc = tc.nc
+    with ExitStack() as ctx:
+        keep = ctx.enter_context(tc.tile_pool(name="keep", bufs=1))
+        pieces = ctx.enter_context(tc.tile_pool(name="pieces", bufs=8))
+        banks = ctx.enter_context(tc.psum_pool(name="banks", bufs=4))
+        held = ctx.enter_context(tc.psum_pool(name="held", bufs=1))
+
+        x_view = xT.rearrange("(s p t) c -> s p t c", p=P, t=PACK)
+        w_view = w.rearrange("(s p t) m -> s p t m", p=P, t=PACK)
+        out_view = out.rearrange("(i m) g -> m i g", m=P)
+
+        pairs = [(s, u) for s in range(PASSES) for u in range(2)]
+        rows = [keep.tile([P, 2, T], F32, name=f"rows{n}") for n in range(len(pairs))]
+        table = [keep.tile([P, T, 2], BF16, name=f"table{n}") for n in range(len(pairs))]
+        w_rows = [keep.tile([P, PACK, M], F32, name=f"w_rows{s}") for s in range(PASSES)]
+        offsets = keep.tile([P, G * K // 16], U16, name="offsets")
+        weights = keep.tile([P, BLOCKS, 8], F32, name="weights")
+        bias_cols = keep.tile([P, CHANNELS], F32, name="bias_cols")
+
+        def load_rows(n, h):
+            s, u = pairs[n]
+            cols = slice(h * HALF, (h + 1) * HALF)
+            nc.sync.dma_start(out=rows[n][:, :, cols], in_=x_view[s, :, 2 * u : 2 * u + 2, cols])
+
+        load_rows(0, 0)
+        nc.sync.dma_start(offsets[:], offs)
+        load_rows(0, 1)
+        nc.sync.dma_start(
+            out=weights[:, :, :K], in_=part[0:1, :].rearrange("o (b g j) -> (o g) b j", b=BLOCKS, j=K)
+        )
+        for n in range(1, len(pairs)):
+            for h in range(2):
+                load_rows(n, h)
+        for s in range(PASSES):
+            nc.sync.dma_start(out=w_rows[s][:], in_=w_view[s])
+        nc.sync.dma_start(out=bias_cols[:], in_=bias.rearrange("(i m) o -> m (i o)", m=P))
+
+        ident = keep.tile([P, P], F32, name="ident")
+        make_identity(nc, ident[:])
+
+        e_values = [
+            [keep.tile([P, P, PACK], BF16, align_bytes=64, name=f"e_values{s}_{b}") for b in range(BLOCKS)]
+            for s in range(PASSES)
+        ]
+        e_codes = [
+            [keep.tile([P, P], U32, align_bytes=64, name=f"e_codes{s}_{b}") for b in range(BLOCKS)]
+            for s in range(PASSES)
+        ]
+        e_scales = [
+            [keep.tile([P, P], U8, align_bytes=64, name=f"e_scales{s}_{b}") for b in range(BLOCKS)]
+            for s in range(PASSES)
+        ]
+        w_values = [keep.tile([P, M, PACK], BF16, align_bytes=64, name=f"w_values{s}") for s in range(PASSES)]
+        w_codes = [keep.tile([P, M], U32, align_bytes=64, name=f"w_codes{s}") for s in range(PASSES)]
+        w_scales = [keep.tile([P, M], U8, align_bytes=64, name=f"w_scales{s}") for s in range(PASSES)]
+        sums = [
+            [held.tile([P, PACK, P], F32, name=f"sums{s}_{b}") for b in range(BLOCKS)] for s in range(PASSES)
+        ]
+        result = keep.tile([P, CHANNELS, G], F32, name="result")
+
+        def cast(n, h, engine):
+            cols = slice(h * HALF, (h + 1) * HALF)
+            src = rows[n][:, :, cols].rearrange("p e c -> p c e")
+            if engine == "scalar":
+                nc.scalar.activation(out=table[n][:, cols, :], in_=src, func=COPY)
+            else:
+                nc.vector.tensor_copy(out=table[n][:, cols, :], in_=src)
+
+        def gather(n, b, bank_corners):
+            words = pieces.tile([P, P, K], U32, name="words")
+            nc.vector.tensor_copy(
+                out=words[:].rearrange("p g j -> p (g j)"),
+                in_=table[n][:]
+                .rearrange("p c e -> p (c e)")
+                .bitcast(U32)
+                .indirect(offsets[:, b * LIST_COLUMNS : (b + 1) * LIST_COLUMNS]),
+            )
+            turned = {}
+            for corners in bank_corners:
+                bank = banks.tile([P, K, P], F32, name="bank")
+                for j in corners:
+                    nc.tensor.transpose(bank[:, j, :], words[:, :, j].bitcast(F32), ident[:])
+                    turned[j] = bank
+            return turned
+
+        def corner(b, turned, j):
+            halves = turned[j][:, j, :].bitcast(BF16).rearrange("g (p e) -> g e p", e=2)
+            return halves, weights[:, b, j : j + 1]
+
+        def add_up(n, b, weighted, slots):
+            s, u = pairs[n]
+            for e in range(2):
+                for j in slots:
+                    nc.tensor.matmul(
+                        sums[s][b][:, 2 * u + e, :],
+                        weighted[:, j, e, :],
+                        ident[:],
+                        start=(j == slots[0]),
+                        stop=(j == slots[-1]),
+                        is_transpose=True,
+                    )
+
+        def weigh(n, b, turned):
+            weighted = pieces.tile([P, K, 2, P], F32, name="weighted")
+            for j in range(K):
+                halves, weight = corner(b, turned, j)
+                nc.scalar.activation(out=weighted[:, j], in_=halves, func=COPY, scale=weight)
+            add_up(n, b, weighted, range(K))
+
+        def weigh_in_twos(n, b, turned):
+            weighted = pieces.tile([P, K, 2, P], F32, name="weighted")
+            for j in (0, 2):
+                halves, weight = corner(b, turned, j)
+                nc.scalar.activation(out=weighted[:, j], in_=halves, func=COPY, scale=weight)
+            for j in (1, 3):
+                halves, weight = corner(b, turned, j)
+                nc.vector.scalar_tensor_tensor(
+                    out=weighted[:, j], in0=halves, scalar=weight, in1=weighted[:, j - 1], op0=MULT, op1=ADD
+                )
+            add_up(n, b, weighted, (1, 3))
+
+        def round_e(s, b):
+            nc.scalar.activation(out=e_values[s][b][:], in_=sums[s][b][:].rearrange("p t g -> p g t"), func=COPY)
+
+        def quantize_e(s, b):
+            nc.vector.quantize_mx(
+                out=e_codes[s][b][:].bitcast(FP8X4),
+                scales=e_scales[s][b][:],
+                in_=e_values[s][b][:].rearrange("p g t -> p (g t)"),
+            )
+
+        def round_w(s):
+            nc.gpsimd.tensor_scalar(
+                out=w_values[s][:],
+                in0=w_rows[s][:].rearrange("p t m -> p m t"),
+                scalar1=1.0,
+                scalar2=0.0,
+                op0=MULT,
+                op1=ADD,
+            )
+
+        def quantize_w(s):
+            nc.vector.quantize_mx(
+                out=w_codes[s][:].bitcast(FP8X4),
+                scales=w_scales[s][:],
+                in_=w_values[s][:].rearrange("p m t -> p (m t)"),
+            )
+
+        def multiply(b, engines):
+            points = slice(b * P, (b + 1) * P)
+            for i in range(CHANNELS):
+                channels = slice(i * P, (i + 1) * P)
+                bank = banks.tile([P, K, P], F32, name="bank")
+                for s in range(PASSES):
+                    nc.tensor.matmul_mx(
+                        out=bank[:, 0, :],
+                        lhsT=w_codes[s][:, channels].bitcast(FP8X4),
+                        lhsT_scale=w_scales[s][:, channels],
+                        rhs=e_codes[s][b][:].bitcast(FP8X4),
+                        rhs_scale=e_scales[s][b][:],
+                        start=(s == 0),
+                        stop=(s == PASSES - 1),
+                    )
+                bias_col = bias_cols[:, i : i + 1]
+                if engines[i] == "scalar":
+                    nc.scalar.activation(
+                        out=result[:, i, points], in_=bank[:, 0, :], func=IDENTITY, bias=bias_col
+                    )
+                else:
+                    nc.vector.tensor_scalar(
+                        out=result[:, i, points], in0=bank[:, 0, :], scalar1=bias_col, scalar2=None, op0=ADD
+                    )
+            nc.sync.dma_start(out=out_view[:, :, points], in_=result[:, :, points])
+
+        one_bank = [(0, 1, 2, 3)]
+        two_banks = [(0, 1), (2, 3)]
+
+        cast(0, 0, "vector")
+        cast(0, 1, "vector")
+        turned_00 = gather(0, 0, two_banks)
+        cast(1, 0, "scalar")
+        turned_01 = gather(0, 1, two_banks)
+        weigh(0, 0, turned_00)
+        cast(1, 1, "vector")
+        weigh(0, 1, turned_01)
+        for s in range(PASSES):
+            round_w(s)
+        cast(2, 0, "vector")
+        turned_10 = gather(1, 0, one_bank)
+        cast(2, 1, "scalar")
+        turned_11 = gather(1, 1, two_banks)
+        cast(3, 0, "scalar")
+        turned_20 = gather(2, 0, one_bank)
+        weigh(1, 0, turned_10)
+        cast(3, 1, "vector")
+        turned_21 = gather(2, 1, one_bank)
+        weigh(1, 1, turned_11)
+        turned_30 = gather(3, 0, one_bank)
+        turned_31 = gather(3, 1, one_bank)
+
+        weigh_in_twos(2, 0, turned_20)
+        round_e(0, 0)
+        weigh_in_twos(2, 1, turned_21)
+        weigh_in_twos(3, 0, turned_30)
+        weigh_in_twos(3, 1, turned_31)
+        round_e(0, 1)
+        quantize_e(0, 0)
+        round_e(1, 0)
+        for s in range(PASSES):
+            quantize_w(s)
+        round_e(1, 1)
+        quantize_e(1, 0)
+        quantize_e(0, 1)
+        quantize_e(1, 1)
+        multiply(0, ("vector", "vector"))
+        multiply(1, ("scalar", "vector"))

@@ -101,9 +101,9 @@ def tile_attend_grid_bias_kernel(tc, xT, w, part, bias, offs, out):
                 nc.vector.tensor_copy(out=table[n][:, cols, :], in_=src)
 
         def gather(n, b, bank_corners):
-            words = pieces.tile([P, P, K], U32, name="words")
+            words = pieces.tile([P, 2, P, 2], U32, name="words")
             nc.vector.tensor_copy(
-                out=words[:].rearrange("p g j -> p (g j)"),
+                out=words[:].rearrange("p h g j -> p g h j"),
                 in_=table[n][:]
                 .rearrange("p c e -> p (c e)")
                 .bitcast(U32)
@@ -113,7 +113,7 @@ def tile_attend_grid_bias_kernel(tc, xT, w, part, bias, offs, out):
             for corners in bank_corners:
                 bank = banks.tile([P, K, P], F32, name="bank")
                 for j in corners:
-                    nc.tensor.transpose(bank[:, j, :], words[:, :, j].bitcast(F32), ident[:])
+                    nc.tensor.transpose(bank[:, j, :], words[:, j // 2, :, j % 2].bitcast(F32), ident[:])
                     turned[j] = bank
             return turned
 

@@ -35,216 +35,260 @@ def tile_attend_grid_bias_kernel(tc, xT, w, part, bias, offs, out):
     nc = tc.nc
     with ExitStack() as ctx:
         keep = ctx.enter_context(tc.tile_pool(name="keep", bufs=1))
-        pieces = ctx.enter_context(tc.tile_pool(name="pieces", bufs=8))
-        banks = ctx.enter_context(tc.psum_pool(name="banks", bufs=4))
-        held = ctx.enter_context(tc.psum_pool(name="held", bufs=1))
+        banks = ctx.enter_context(tc.psum_pool(name="banks", bufs=1))
+
+        def bank(name, on):
+            return banks.tile([P, K, P], F32, name=name, tag=on)
+
+        def sbuf(shape, dtype, name, on=None):
+            return keep.tile(shape, dtype, align_bytes=64, name=name, tag=on or name)
 
         x_view = xT.rearrange("(s p t) c -> s p t c", p=P, t=PACK)
-        w_view = w.rearrange("(s p t) m -> s p t m", p=P, t=PACK)
+        w_view = w.rearrange("(s p t) m -> p s t m", p=P, t=PACK)
         out_view = out.rearrange("(i m) g -> m i g", m=P)
 
         pairs = [(s, u) for s in range(PASSES) for u in range(2)]
-        rows = [keep.tile([P, 2, T], F32, name=f"rows{n}") for n in range(len(pairs))]
-        table = [keep.tile([P, T, 2], BF16, name=f"table{n}") for n in range(len(pairs))]
-        w_rows = [keep.tile([P, PACK, M], F32, name=f"w_rows{s}") for s in range(PASSES)]
+        table = [sbuf([P, T], F32, f"table{n}") for n in range(len(pairs))]
+        cuts = [[0, HALF, HALF + HALF // 2, T], [0, HALF, T], [0, HALF, T], [0, T]]
+        spans = [[slice(a, z) for a, z in zip(c, c[1:])] for c in cuts]
+        low_rows = {}
         offsets = keep.tile([P, G * K // 16], U16, name="offsets")
         weights = keep.tile([P, BLOCKS, 8], F32, name="weights")
-        bias_cols = keep.tile([P, CHANNELS], F32, name="bias_cols")
 
-        def load_rows(n, h):
+        def load_high(n):
             s, u = pairs[n]
-            cols = slice(h * HALF, (h + 1) * HALF)
-            nc.sync.dma_start(out=rows[n][:, :, cols], in_=x_view[s, :, 2 * u : 2 * u + 2, cols])
+            nc.sync.dma_start(out=table[n][:], in_=x_view[s, :, 2 * u + 1, :])
 
-        load_rows(0, 0)
-        nc.sync.dma_start(offsets[:], offs)
-        load_rows(0, 1)
-        nc.sync.dma_start(
+        def load_low(n, h, on=None):
+            s, u = pairs[n]
+            cols = spans[n][h]
+            low_rows[n, h] = sbuf([P, cols.stop - cols.start], F32, f"low{n}_{h}", on)
+            nc.sync.dma_start(out=low_rows[n, h][:], in_=x_view[s, :, 2 * u, cols])
+
+        nc.scalar.dma_start(
             out=weights[:, :, :K], in_=part[0:1, :].rearrange("o (b g j) -> (o g) b j", b=BLOCKS, j=K)
         )
-        for n in range(1, len(pairs)):
-            for h in range(2):
-                load_rows(n, h)
-        for s in range(PASSES):
-            nc.sync.dma_start(out=w_rows[s][:], in_=w_view[s])
+        w_whole = sbuf([P, PASSES, PACK, M], F32, "w_rows")
+        bias_cols = sbuf([P, CHANNELS], F32, "bias_cols")
+        for n in range(len(pairs)):
+            load_high(n)
+            for h in range(len(spans[n])):
+                load_low(n, h)
+            if n == 0:
+                nc.sync.dma_start(offsets[:], offs)
+        nc.sync.dma_start(out=w_whole[:], in_=w_view)
         nc.sync.dma_start(out=bias_cols[:], in_=bias.rearrange("(i m) o -> m (i o)", m=P))
 
         ident = keep.tile([P, P], F32, name="ident")
-        make_identity(nc, ident[:])
+        nc.vector.memset(ident[:], 0.0)
+        make_identity(nc, ident[:], nomemset=True)
+        warm = keep.tile([P, 2], F32, name="warm")
+        nc.vector.memset(warm[:, 0:1], 0.0)
+        nc.scalar.activation(out=warm[:, 1:2], in_=warm[:, 0:1], func=COPY)
 
-        e_values = [
-            [keep.tile([P, P, PACK], BF16, align_bytes=64, name=f"e_values{s}_{b}") for b in range(BLOCKS)]
-            for s in range(PASSES)
-        ]
-        e_codes = [
-            [keep.tile([P, P], U32, align_bytes=64, name=f"e_codes{s}_{b}") for b in range(BLOCKS)]
-            for s in range(PASSES)
-        ]
-        e_scales = [
-            [keep.tile([P, P], U8, align_bytes=64, name=f"e_scales{s}_{b}") for b in range(BLOCKS)]
-            for s in range(PASSES)
-        ]
-        w_values = [keep.tile([P, M, PACK], BF16, align_bytes=64, name=f"w_values{s}") for s in range(PASSES)]
-        w_codes = [keep.tile([P, M], U32, align_bytes=64, name=f"w_codes{s}") for s in range(PASSES)]
-        w_scales = [keep.tile([P, M], U8, align_bytes=64, name=f"w_scales{s}") for s in range(PASSES)]
-        sums = [
-            [held.tile([P, PACK, P], F32, name=f"sums{s}_{b}") for b in range(BLOCKS)] for s in range(PASSES)
-        ]
-        result = keep.tile([P, CHANNELS, G], F32, name="result")
+        e_values = [sbuf([P, G, PACK], BF16, f"e_values{s}") for s in range(PASSES)]
+        e_codes = [sbuf([P, G], U32, f"e_codes{s}") for s in range(PASSES)]
+        w_codes = sbuf([P, PASSES * M], U32, "w_codes")
+        sums = {(s, b): bank(f"sums{s}_{b}", f"sums{s}_{b}") for s in range(PASSES) for b in range(BLOCKS)}
+        words = {}
+        turned = {}
+        w_scales = {}
+        e_scales = {}
+        seen = {}
 
         def cast(n, h, engine):
-            cols = slice(h * HALF, (h + 1) * HALF)
-            src = rows[n][:, :, cols].rearrange("p e c -> p c e")
+            low_halves = table[n][:].bitcast(BF16).rearrange("p (c e) -> p c e", e=2)[:, spans[n][h], 0]
             if engine == "scalar":
-                nc.scalar.activation(out=table[n][:, cols, :], in_=src, func=COPY)
+                nc.scalar.activation(out=low_halves, in_=low_rows[n, h][:], func=COPY)
             else:
-                nc.vector.tensor_copy(out=table[n][:, cols, :], in_=src)
+                nc.vector.tensor_copy(out=low_halves, in_=low_rows[n, h][:])
 
-        def gather(n, b, bank_corners):
-            words = pieces.tile([P, 2, P, 2], U32, name="words")
+        def gather(n, b, on=None):
+            words[n, b] = sbuf([P, 2, P, 2], U32, f"words{n}_{b}", on)
             nc.vector.tensor_copy(
-                out=words[:].rearrange("p h g j -> p g h j"),
-                in_=table[n][:]
-                .rearrange("p c e -> p (c e)")
-                .bitcast(U32)
-                .indirect(offsets[:, b * LIST_COLUMNS : (b + 1) * LIST_COLUMNS]),
+                out=words[n, b][:].rearrange("p h g j -> p g h j"),
+                in_=table[n][:].bitcast(U32).indirect(offsets[:, b * LIST_COLUMNS : (b + 1) * LIST_COLUMNS]),
             )
-            turned = {}
-            for corners in bank_corners:
-                bank = banks.tile([P, K, P], F32, name="bank")
-                for j in corners:
-                    nc.tensor.transpose(bank[:, j, :], words[:, j // 2, :, j % 2].bitcast(F32), ident[:])
-                    turned[j] = bank
-            return turned
 
-        def corner(b, turned, j):
-            halves = turned[j][:, j, :].bitcast(BF16).rearrange("g (p e) -> g e p", e=2)
+        def turn(n, b, on, corners=range(K)):
+            into = bank(f"turned{n}_{b}_{corners[0]}", on)
+            for j in corners:
+                nc.tensor.transpose(into[:, j, :], words[n, b][:, j // 2, :, j % 2].bitcast(F32), ident[:])
+                turned[n, b, j] = into
+
+        def corner(n, b, j):
+            halves = turned[n, b, j][:, j, :].bitcast(BF16).rearrange("g (p e) -> g e p", e=2)
             return halves, weights[:, b, j : j + 1]
 
-        def add_up(n, b, weighted, slots):
+        def add_up(n, b, weighted, count):
             s, u = pairs[n]
+            slots = weighted if isinstance(weighted, list) else [weighted[:, j] for j in range(count)]
             for e in range(2):
-                for j in slots:
+                for j in range(count):
                     nc.tensor.matmul(
-                        sums[s][b][:, 2 * u + e, :],
-                        weighted[:, j, e, :],
+                        sums[s, b][:, 2 * u + e, :],
+                        slots[j][:, e, :],
                         ident[:],
-                        start=(j == slots[0]),
-                        stop=(j == slots[-1]),
+                        start=(j == 0),
+                        stop=(j == count - 1),
                         is_transpose=True,
                     )
 
-        def weigh(n, b, turned):
-            weighted = pieces.tile([P, K, 2, P], F32, name="weighted")
+        def weigh_four(n, b, on=None):
+            weighted = sbuf([P, K, 2, P], F32, f"weighted{n}_{b}", on)
             for j in range(K):
-                halves, weight = corner(b, turned, j)
+                halves, weight = corner(n, b, j)
                 nc.scalar.activation(out=weighted[:, j], in_=halves, func=COPY, scale=weight)
-            add_up(n, b, weighted, range(K))
+            return weighted
 
-        def weigh_in_twos(n, b, turned):
-            weighted = pieces.tile([P, K, 2, P], F32, name="weighted")
-            for j in (0, 2):
-                halves, weight = corner(b, turned, j)
-                nc.scalar.activation(out=weighted[:, j], in_=halves, func=COPY, scale=weight)
-            for j in (1, 3):
-                halves, weight = corner(b, turned, j)
+        def weigh_two(n, b, h, on):
+            weighted = sbuf([P, 2, 2, P], F32, f"weighted{n}_{b}_{h}", on)
+            for i in range(2):
+                halves, weight = corner(n, b, 2 * h + i)
+                nc.scalar.activation(out=weighted[:, i], in_=halves, func=COPY, scale=weight)
+            return [weighted[:, i] for i in range(2)]
+
+        def weigh(n, b, on=None):
+            add_up(n, b, weigh_four(n, b, on), K)
+
+        def weigh_even(n, b, on=None):
+            even = sbuf([P, 2, 2, P], F32, f"even{n}_{b}", on)
+            for i in range(2):
+                halves, weight = corner(n, b, 2 * i)
+                nc.scalar.activation(out=even[:, i], in_=halves, func=COPY, scale=weight)
+            return even
+
+        def weigh_odd(n, b, even, on=None):
+            twos = sbuf([P, 2, 2, P], F32, f"twos{n}_{b}", on)
+            for i in range(2):
+                halves, weight = corner(n, b, 2 * i + 1)
                 nc.vector.scalar_tensor_tensor(
-                    out=weighted[:, j], in0=halves, scalar=weight, in1=weighted[:, j - 1], op0=MULT, op1=ADD
+                    out=twos[:, i], in0=halves, scalar=weight, in1=even[:, i], op0=MULT, op1=ADD
                 )
-            add_up(n, b, weighted, (1, 3))
+            return twos
+
+        def weigh_side_by_side(n, b):
+            weighted = sbuf([P, 3, 2, P], F32, f"weighted{n}_{b}")
+            third = sbuf([P, 2, P], F32, f"third{n}_{b}")
+            for j in range(2):
+                halves, weight = corner(n, b, j)
+                nc.scalar.activation(out=weighted[:, j], in_=halves, func=COPY, scale=weight)
+            halves, weight = corner(n, b, 2)
+            nc.vector.tensor_scalar(out=third[:], in0=halves, scalar1=weight, scalar2=None, op0=MULT)
+            halves, weight = corner(n, b, 3)
+            nc.vector.scalar_tensor_tensor(
+                out=weighted[:, 2], in0=halves, scalar=weight, in1=third[:], op0=MULT, op1=ADD
+            )
+            add_up(n, b, weighted, 3)
+            seen[n, b] = weighted
+
+        def weigh_alone(n, b, on):
+            even = sbuf([P, 2, 2, P], F32, f"even{n}_{b}", on)
+            for i in range(2):
+                halves, weight = corner(n, b, 2 * i)
+                nc.vector.tensor_scalar(out=even[:, i], in0=halves, scalar1=weight, scalar2=None, op0=MULT)
+            return weigh_odd(n, b, even)
 
         def round_e(s, b):
-            nc.scalar.activation(out=e_values[s][b][:], in_=sums[s][b][:].rearrange("p t g -> p g t"), func=COPY)
-
-        def quantize_e(s, b):
-            nc.vector.quantize_mx(
-                out=e_codes[s][b][:].bitcast(FP8X4),
-                scales=e_scales[s][b][:],
-                in_=e_values[s][b][:].rearrange("p g t -> p (g t)"),
+            points = slice(b * P, (b + 1) * P)
+            nc.scalar.activation(
+                out=e_values[s][:, points, :], in_=sums[s, b][:].rearrange("p t g -> p g t"), func=COPY
             )
 
-        def round_w(s):
+        def quantize_e(s, points, on=None):
+            if s not in e_scales:
+                e_scales[s] = sbuf([P, G], U8, f"e_scales{s}", on)
+            nc.vector.quantize_mx(
+                out=e_codes[s][:, points].bitcast(FP8X4),
+                scales=e_scales[s][:, points],
+                in_=e_values[s][:, points, :].rearrange("p g t -> p (g t)"),
+            )
+
+        def round_w_whole(on):
+            w_values = sbuf([P, PASSES, M, PACK], BF16, "w_values", on)
             nc.gpsimd.tensor_scalar(
-                out=w_values[s][:],
-                in0=w_rows[s][:].rearrange("p t m -> p m t"),
-                scalar1=1.0,
-                scalar2=0.0,
-                op0=MULT,
-                op1=ADD,
+                out=w_values[:], in0=w_whole[:].rearrange("p s t m -> p s m t"), scalar1=1.0, scalar2=0.0, op0=MULT, op1=ADD
             )
+            return w_values
 
-        def quantize_w(s):
+        def quantize_w_whole(w_values, on):
+            scales = sbuf([P, PASSES * M], U8, "w_scales", on)
+            for s in range(PASSES):
+                w_scales[s] = scales[:, s * M : (s + 1) * M]
             nc.vector.quantize_mx(
-                out=w_codes[s][:].bitcast(FP8X4),
-                scales=w_scales[s][:],
-                in_=w_values[s][:].rearrange("p m t -> p (m t)"),
+                out=w_codes[:].bitcast(FP8X4), scales=scales[:], in_=w_values[:].rearrange("p s m t -> p (s m t)")
             )
 
-        def multiply(b, engines):
+        def multiply(s, b):
             points = slice(b * P, (b + 1) * P)
             for i in range(CHANNELS):
-                channels = slice(i * P, (i + 1) * P)
-                bank = banks.tile([P, K, P], F32, name="bank")
-                for s in range(PASSES):
-                    nc.tensor.matmul_mx(
-                        out=bank[:, 0, :],
-                        lhsT=w_codes[s][:, channels].bitcast(FP8X4),
-                        lhsT_scale=w_scales[s][:, channels],
-                        rhs=e_codes[s][b][:].bitcast(FP8X4),
-                        rhs_scale=e_scales[s][b][:],
-                        start=(s == 0),
-                        stop=(s == PASSES - 1),
-                    )
-                bias_col = bias_cols[:, i : i + 1]
-                if engines[i] == "scalar":
-                    nc.scalar.activation(
-                        out=result[:, i, points], in_=bank[:, 0, :], func=IDENTITY, bias=bias_col
-                    )
-                else:
-                    nc.vector.tensor_scalar(
-                        out=result[:, i, points], in0=bank[:, 0, :], scalar1=bias_col, scalar2=None, op0=ADD
-                    )
-            nc.sync.dma_start(out=out_view[:, :, points], in_=result[:, :, points])
+                channels = slice(s * M + i * P, s * M + (i + 1) * P)
+                nc.tensor.matmul_mx(
+                    out=products[b][i][:, 0, :],
+                    lhsT=w_codes[:, channels].bitcast(FP8X4),
+                    lhsT_scale=w_scales[s][:, i * P : (i + 1) * P],
+                    rhs=e_codes[s][:, points].bitcast(FP8X4),
+                    rhs_scale=e_scales[s][:, points],
+                    start=(s == 0),
+                    stop=(s == PASSES - 1),
+                )
 
-        one_bank = [(0, 1, 2, 3)]
-        two_banks = [(0, 1), (2, 3)]
+        def finish(b, on=None):
+            points = slice(b * P, (b + 1) * P)
+            result = sbuf([P, CHANNELS, P], F32, f"result{b}", on)
+            nc.scalar.activation(out=result[:, 0], in_=products[b][0][:, 0, :], func=IDENTITY, bias=bias_cols[:, 0:1])
+            nc.vector.tensor_scalar(
+                out=result[:, 1], in0=products[b][1][:, 0, :], scalar1=bias_cols[:, 1:2], scalar2=None, op0=ADD
+            )
+            nc.sync.dma_start(out=out_view[:, :, points], in_=result[:])
 
-        cast(0, 0, "vector")
-        cast(0, 1, "vector")
-        turned_00 = gather(0, 0, two_banks)
+        for h in range(3):
+            cast(0, h, "vector")
+        gather(0, 0)
+        gather(0, 1)
         cast(1, 0, "scalar")
-        turned_01 = gather(0, 1, two_banks)
-        weigh(0, 0, turned_00)
         cast(1, 1, "vector")
-        weigh(0, 1, turned_01)
-        for s in range(PASSES):
-            round_w(s)
-        cast(2, 0, "vector")
-        turned_10 = gather(1, 0, one_bank)
-        cast(2, 1, "scalar")
-        turned_11 = gather(1, 1, two_banks)
+        gather(1, 0)
+        gather(1, 1)
+        cast(2, 1, "vector")
+        turn(0, 0, "a")
+        turn(0, 1, "b")
+        weigh(0, 0, on="low1_0")
+        turn(1, 0, "a")
+        weigh(0, 1)
+        cast(2, 0, "scalar")
+        gather(2, 0)
+        gather(2, 1)
+        turn(1, 1, "b")
+        weigh(1, 0, on="low2_0")
         cast(3, 0, "scalar")
-        turned_20 = gather(2, 0, one_bank)
-        weigh(1, 0, turned_10)
-        cast(3, 1, "vector")
-        turned_21 = gather(2, 1, one_bank)
-        weigh(1, 1, turned_11)
-        turned_30 = gather(3, 0, one_bank)
-        turned_31 = gather(3, 1, one_bank)
-
-        weigh_in_twos(2, 0, turned_20)
+        gather(3, 0)
+        gather(3, 1)
+        w_values = round_w_whole("table3")
+        turn(2, 0, "c")
+        turn(2, 1, "a")
+        turn(3, 0, "d")
+        weigh(1, 1, on="low3_0")
+        turn(3, 1, "b")
+        even_20 = weigh_even(2, 0, on="weighted1_0")
+        even_21 = weigh_even(2, 1)
         round_e(0, 0)
-        weigh_in_twos(2, 1, turned_21)
-        weigh_in_twos(3, 0, turned_30)
-        weigh_in_twos(3, 1, turned_31)
+        even_30 = weigh_even(3, 0)
+        twos_20 = weigh_odd(2, 0, even_20, "table2")
+        add_up(2, 0, twos_20, 2)
+        add_up(2, 1, weigh_odd(2, 1, even_21), 2)
+        add_up(3, 0, weigh_odd(3, 0, even_30), 2)
+        add_up(3, 1, weigh_odd(3, 1, weigh_even(3, 1)), 2)
         round_e(0, 1)
-        quantize_e(0, 0)
         round_e(1, 0)
-        for s in range(PASSES):
-            quantize_w(s)
         round_e(1, 1)
-        quantize_e(1, 0)
-        quantize_e(0, 1)
-        quantize_e(1, 1)
-        multiply(0, ("vector", "vector"))
-        multiply(1, ("scalar", "vector"))
+        quantize_w_whole(w_values, "even3_1")
+        quantize_e(0, slice(0, G), "table3")
+        quantize_e(1, slice(0, P))
+        quantize_e(1, slice(P, G))
+        products = [[bank(f"products{b}_{i}", on) for i, on in enumerate(ons)] for b, ons in enumerate((("sums0_0", "sums0_1"), ("a", "d")))]
+        for s in range(PASSES):
+            for b in range(BLOCKS):
+                multiply(s, b)
+        finish(0, "e_values1")
+        finish(1)

@@ -49,7 +49,7 @@ def tile_attend_grid_bias_kernel(tc, xT, w, part, bias, offs, out):
 
         pairs = [(s, u) for s in range(PASSES) for u in range(2)]
         table = [sbuf([P, T], F32, f"table{n}") for n in range(len(pairs))]
-        cuts = [[0, HALF, HALF + HALF // 2, T], [0, HALF, T], [0, HALF, T], [0, T]]
+        cuts = [[0, HALF, HALF + HALF // 2, T], [0, HALF, T], [0, T], [0, HALF + HALF // 2, T]]
         spans = [[slice(a, z) for a, z in zip(c, c[1:])] for c in cuts]
         low_rows = {}
         offsets = keep.tile([P, G * K // 16], U16, name="offsets")
@@ -147,6 +147,11 @@ def tile_attend_grid_bias_kernel(tc, xT, w, part, bias, offs, out):
                 halves, weight = corner(n, b, 2 * h + i)
                 nc.scalar.activation(out=weighted[:, i], in_=halves, func=COPY, scale=weight)
             return [weighted[:, i] for i in range(2)]
+
+        def add_pairs(n, b, weighted):
+            twos = sbuf([P, 2, 2, P], F32, f"twos{n}_{b}")
+            nc.gpsimd.tensor_tensor(out=twos[:], in0=weighted[:, 0:2], in1=weighted[:, 2:4], op=ADD)
+            add_up(n, b, twos, 2)
 
         def weigh(n, b, on=None):
             add_up(n, b, weigh_four(n, b, on), K)
@@ -250,29 +255,35 @@ def tile_attend_grid_bias_kernel(tc, xT, w, part, bias, offs, out):
         cast(1, 1, "vector")
         gather(1, 0)
         gather(1, 1)
-        cast(2, 1, "vector")
-        turn(0, 0, "a")
-        turn(0, 1, "b")
-        weigh(0, 0, on="low1_0")
-        turn(1, 0, "a")
-        weigh(0, 1)
-        cast(2, 0, "scalar")
+        cast(2, 0, "vector")
         gather(2, 0)
         gather(2, 1)
-        turn(1, 1, "b")
-        weigh(1, 0, on="low2_0")
+        turn(0, 0, "a", (0, 1))
+        turn(0, 0, "c", (2, 3))
+        turn(0, 1, "b")
+        weighted = weigh_four(0, 0, on="low1_0")
+        add_up(0, 0, weighted, K)
+        turn(1, 0, "a")
+        turn(1, 1, "c", (2, 3))
+        weighted = weigh_four(0, 1, on=None)
+        add_up(0, 1, weighted, K)
+        turn(1, 1, "b", (0, 1))
+        weighted = weigh_four(1, 0, on=None)
+        add_up(1, 0, weighted, K)
+        turn(2, 0, "a")
         cast(3, 0, "scalar")
+        cast(3, 1, "scalar")
         gather(3, 0)
         gather(3, 1)
-        w_values = round_w_whole("table3")
-        turn(2, 0, "c")
-        turn(2, 1, "a")
-        turn(3, 0, "d")
-        weigh(1, 1, on="low3_0")
-        turn(3, 1, "b")
-        even_20 = weigh_even(2, 0, on="weighted1_0")
-        even_21 = weigh_even(2, 1)
+        weighted = weigh_four(1, 1, on="low3_0")
+        add_up(1, 1, weighted, K)
+        turn(2, 1, "b")
+        turn(3, 0, "c")
+        w_values = round_w_whole(None)
+        even_20 = weigh_even(2, 0, on="low3_1")
         round_e(0, 0)
+        turn(3, 1, "sums0_0")
+        even_21 = weigh_even(2, 1)
         even_30 = weigh_even(3, 0)
         twos_20 = weigh_odd(2, 0, even_20, "table2")
         add_up(2, 0, twos_20, 2)
@@ -282,11 +293,11 @@ def tile_attend_grid_bias_kernel(tc, xT, w, part, bias, offs, out):
         round_e(0, 1)
         round_e(1, 0)
         round_e(1, 1)
-        quantize_w_whole(w_values, "even3_1")
-        quantize_e(0, slice(0, G), "table3")
+        quantize_w_whole(w_values, "even3_0")
+        quantize_e(0, slice(0, G), "w_values")
         quantize_e(1, slice(0, P))
         quantize_e(1, slice(P, G))
-        products = [[bank(f"products{b}_{i}", on) for i, on in enumerate(ons)] for b, ons in enumerate((("sums0_0", "sums0_1"), ("a", "d")))]
+        products = [[bank(f"products{b}_{i}", on) for i, on in enumerate(ons)] for b, ons in enumerate((("d", "sums0_1"), ("b", "c")))]
         for s in range(PASSES):
             for b in range(BLOCKS):
                 multiply(s, b)

@@ -48,22 +48,18 @@ def tile_attend_grid_bias_kernel(tc, xT, w, part, bias, offs, out):
         out_view = out.rearrange("(i m) g -> m i g", m=P)
 
         pairs = [(s, u) for s in range(PASSES) for u in range(2)]
-        table = [sbuf([P, T], F32, f"table{n}") for n in range(len(pairs))]
-        cuts = [[0, HALF, HALF + HALF // 2, T], [0, HALF, T], [0, T], [0, HALF + HALF // 2, T]]
+        table = [sbuf([P, T, 2], BF16, f"table{n}") for n in range(len(pairs))]
+        cuts = [[0, HALF, HALF + HALF // 2, T], [0, HALF, T], [0, HALF, T], [0, HALF, T]]
         spans = [[slice(a, z) for a, z in zip(c, c[1:])] for c in cuts]
         low_rows = {}
         offsets = keep.tile([P, G * K // 16], U16, name="offsets")
         weights = keep.tile([P, BLOCKS, 8], F32, name="weights")
 
-        def load_high(n):
-            s, u = pairs[n]
-            nc.sync.dma_start(out=table[n][:], in_=x_view[s, :, 2 * u + 1, :])
-
         def load_low(n, h, on=None):
             s, u = pairs[n]
             cols = spans[n][h]
-            low_rows[n, h] = sbuf([P, cols.stop - cols.start], F32, f"low{n}_{h}", on)
-            nc.sync.dma_start(out=low_rows[n, h][:], in_=x_view[s, :, 2 * u, cols])
+            low_rows[n, h] = sbuf([P, 2, cols.stop - cols.start], F32, f"low{n}_{h}", on)
+            nc.sync.dma_start(out=low_rows[n, h][:], in_=x_view[s, :, 2 * u : 2 * u + 2, cols])
 
         nc.scalar.dma_start(
             out=weights[:, :, :K], in_=part[0:1, :].rearrange("o (b g j) -> (o g) b j", b=BLOCKS, j=K)
@@ -71,7 +67,6 @@ def tile_attend_grid_bias_kernel(tc, xT, w, part, bias, offs, out):
         w_whole = sbuf([P, PASSES, PACK, M], F32, "w_rows")
         bias_cols = sbuf([P, CHANNELS], F32, "bias_cols")
         for n in range(len(pairs)):
-            load_high(n)
             for h in range(len(spans[n])):
                 load_low(n, h)
             if n == 0:
@@ -82,9 +77,6 @@ def tile_attend_grid_bias_kernel(tc, xT, w, part, bias, offs, out):
         ident = keep.tile([P, P], F32, name="ident")
         nc.vector.memset(ident[:], 0.0)
         make_identity(nc, ident[:], nomemset=True)
-        warm = keep.tile([P, 2], F32, name="warm")
-        nc.vector.memset(warm[:, 0:1], 0.0)
-        nc.scalar.activation(out=warm[:, 1:2], in_=warm[:, 0:1], func=COPY)
 
         e_values = [sbuf([P, G, PACK], BF16, f"e_values{s}") for s in range(PASSES)]
         e_codes = [sbuf([P, G], U32, f"e_codes{s}") for s in range(PASSES)]
@@ -97,17 +89,25 @@ def tile_attend_grid_bias_kernel(tc, xT, w, part, bias, offs, out):
         seen = {}
 
         def cast(n, h, engine):
-            low_halves = table[n][:].bitcast(BF16).rearrange("p (c e) -> p c e", e=2)[:, spans[n][h], 0]
+            src = low_rows[n, h][:].rearrange("p e c -> p c e")
             if engine == "scalar":
-                nc.scalar.activation(out=low_halves, in_=low_rows[n, h][:], func=COPY)
+                nc.scalar.activation(out=table[n][:, spans[n][h], :], in_=src, func=COPY)
             else:
-                nc.vector.tensor_copy(out=low_halves, in_=low_rows[n, h][:])
+                nc.vector.tensor_copy(out=table[n][:, spans[n][h], :], in_=src)
 
         def gather(n, b, on=None):
             words[n, b] = sbuf([P, 2, P, 2], U32, f"words{n}_{b}", on)
             nc.vector.tensor_copy(
                 out=words[n, b][:].rearrange("p h g j -> p g h j"),
-                in_=table[n][:].bitcast(U32).indirect(offsets[:, b * LIST_COLUMNS : (b + 1) * LIST_COLUMNS]),
+                in_=table[n][:].rearrange("p c e -> p (c e)").bitcast(U32).indirect(offsets[:, b * LIST_COLUMNS : (b + 1) * LIST_COLUMNS]),
+            )
+
+        def gather_plain(n, b):
+            plain = sbuf([P, P, 2, 2], U32, f"words{n}_{b}")
+            words[n, b] = plain[:].rearrange("p g h j -> p h g j")
+            nc.vector.tensor_copy(
+                out=plain[:].rearrange("p g h j -> p (g h j)"),
+                in_=table[n][:].rearrange("p c e -> p (c e)").bitcast(U32).indirect(offsets[:, b * LIST_COLUMNS : (b + 1) * LIST_COLUMNS]),
             )
 
         def turn(n, b, on, corners=range(K)):
@@ -156,8 +156,8 @@ def tile_attend_grid_bias_kernel(tc, xT, w, part, bias, offs, out):
         def weigh(n, b, on=None):
             add_up(n, b, weigh_four(n, b, on), K)
 
-        def weigh_even(n, b, on=None):
-            even = sbuf([P, 2, 2, P], F32, f"even{n}_{b}", on)
+        def weigh_even(n, b, on=None, into=None):
+            even = sbuf([P, 2, 2, P], F32, f"even{n}_{b}", on) if into is None else into
             for i in range(2):
                 halves, weight = corner(n, b, 2 * i)
                 nc.scalar.activation(out=even[:, i], in_=halves, func=COPY, scale=weight)
@@ -247,57 +247,57 @@ def tile_attend_grid_bias_kernel(tc, xT, w, part, bias, offs, out):
             )
             nc.sync.dma_start(out=out_view[:, :, points], in_=result[:])
 
-        for h in range(3):
+        for h in range(len(spans[0])):
             cast(0, h, "vector")
-        gather(0, 0)
-        gather(0, 1)
+        gather_plain(0, 0)
+        gather_plain(0, 1)
         cast(1, 0, "scalar")
         cast(1, 1, "vector")
-        gather(1, 0)
-        gather(1, 1)
         cast(2, 0, "vector")
-        gather(2, 0)
-        gather(2, 1)
+        gather_plain(1, 0)
+        gather_plain(1, 1)
         turn(0, 0, "a", (0, 1))
         turn(0, 0, "c", (2, 3))
-        turn(0, 1, "b")
+        turn(0, 1, "b", (0, 1))
+        turn(0, 1, "d", (2, 3))
         weighted = weigh_four(0, 0, on="low1_0")
-        add_up(0, 0, weighted, K)
         turn(1, 0, "a")
-        turn(1, 1, "c", (2, 3))
-        weighted = weigh_four(0, 1, on=None)
+        add_up(0, 0, weighted, K)
+        weighted = weigh_four(0, 1)
+        turn(1, 1, "b")
         add_up(0, 1, weighted, K)
-        turn(1, 1, "b", (0, 1))
-        weighted = weigh_four(1, 0, on=None)
-        add_up(1, 0, weighted, K)
-        turn(2, 0, "a")
-        cast(3, 0, "scalar")
-        cast(3, 1, "scalar")
+        cast(2, 1, "scalar")
+        gather_plain(2, 0)
+        gather_plain(2, 1)
+        turn(2, 0, "c")
+        turn(2, 1, "d")
+        for h in range(len(spans[3])):
+            cast(3, h, "scalar")
         gather(3, 0)
         gather(3, 1)
-        weighted = weigh_four(1, 1, on="low3_0")
-        add_up(1, 1, weighted, K)
-        turn(2, 1, "b")
-        turn(3, 0, "c")
         w_values = round_w_whole(None)
-        even_20 = weigh_even(2, 0, on="low3_1")
-        round_e(0, 0)
-        turn(3, 1, "sums0_0")
+        weighted = weigh_four(1, 0, on="low3_0")
+        turn(3, 0, "a")
+        add_up(1, 0, weighted, K)
+        weighted = weigh_four(1, 1, on="low3_1")
+        turn(3, 1, "b")
+        add_up(1, 1, weighted, K)
+        even_20 = weigh_even(2, 0)
         even_21 = weigh_even(2, 1)
         even_30 = weigh_even(3, 0)
-        twos_20 = weigh_odd(2, 0, even_20, "table2")
-        add_up(2, 0, twos_20, 2)
+        add_up(2, 0, weigh_odd(2, 0, even_20), 2)
         add_up(2, 1, weigh_odd(2, 1, even_21), 2)
         add_up(3, 0, weigh_odd(3, 0, even_30), 2)
         add_up(3, 1, weigh_odd(3, 1, weigh_even(3, 1)), 2)
+        round_e(0, 0)
         round_e(0, 1)
         round_e(1, 0)
         round_e(1, 1)
         quantize_w_whole(w_values, "even3_0")
-        quantize_e(0, slice(0, G), "w_values")
+        quantize_e(0, slice(0, G), "even3_1")
         quantize_e(1, slice(0, P))
         quantize_e(1, slice(P, G))
-        products = [[bank(f"products{b}_{i}", on) for i, on in enumerate(ons)] for b, ons in enumerate((("d", "sums0_1"), ("b", "c")))]
+        products = [[bank(f"products{b}_{i}", on) for i, on in enumerate(ons)] for b, ons in enumerate((("sums0_0", "sums0_1"), ("c", "d")))]
         for s in range(PASSES):
             for b in range(BLOCKS):
                 multiply(s, b)

@@ -102,14 +102,6 @@ def tile_attend_grid_bias_kernel(tc, xT, w, part, bias, offs, out):
                 in_=table[n][:].rearrange("p c e -> p (c e)").bitcast(U32).indirect(offsets[:, b * LIST_COLUMNS : (b + 1) * LIST_COLUMNS]),
             )
 
-        def gather_plain(n, b):
-            plain = sbuf([P, P, 2, 2], U32, f"words{n}_{b}")
-            words[n, b] = plain[:].rearrange("p g h j -> p h g j")
-            nc.vector.tensor_copy(
-                out=plain[:].rearrange("p g h j -> p (g h j)"),
-                in_=table[n][:].rearrange("p c e -> p (c e)").bitcast(U32).indirect(offsets[:, b * LIST_COLUMNS : (b + 1) * LIST_COLUMNS]),
-            )
-
         def turn(n, b, on, corners=range(K)):
             into = bank(f"turned{n}_{b}_{corners[0]}", on)
             for j in corners:
@@ -249,13 +241,13 @@ def tile_attend_grid_bias_kernel(tc, xT, w, part, bias, offs, out):
 
         for h in range(len(spans[0])):
             cast(0, h, "vector")
-        gather_plain(0, 0)
-        gather_plain(0, 1)
+        gather(0, 0)
+        gather(0, 1)
         cast(1, 0, "scalar")
         cast(1, 1, "vector")
         cast(2, 0, "vector")
-        gather_plain(1, 0)
-        gather_plain(1, 1)
+        gather(1, 0)
+        gather(1, 1)
         turn(0, 0, "a", (0, 1))
         turn(0, 0, "c", (2, 3))
         turn(0, 1, "b", (0, 1))
@@ -267,8 +259,8 @@ def tile_attend_grid_bias_kernel(tc, xT, w, part, bias, offs, out):
         turn(1, 1, "b")
         add_up(0, 1, weighted, K)
         cast(2, 1, "scalar")
-        gather_plain(2, 0)
-        gather_plain(2, 1)
+        gather(2, 0)
+        gather(2, 1)
         turn(2, 0, "c")
         turn(2, 1, "d")
         for h in range(len(spans[3])):

@@ -1,7 +1,6 @@
 from contextlib import ExitStack
 
 import concourse.mybir as mybir
-from concourse.masks import make_identity
 
 F32 = mybir.dt.float32
 BF16 = mybir.dt.bfloat16
@@ -11,6 +10,7 @@ U8 = mybir.dt.uint8
 FP8X4 = mybir.dt.float8_e4m3fn_x4
 COPY = mybir.ActivationFunctionType.Copy
 IDENTITY = mybir.ActivationFunctionType.Identity
+EQUAL = mybir.AluOpType.is_equal
 ADD = mybir.AluOpType.add
 MULT = mybir.AluOpType.mult
 
@@ -24,9 +24,13 @@ PACK = 4
 PASSES = D // (P * PACK)
 BLOCKS = G // P
 CHANNELS = M // P
+QUADRANT = 32
 HALF = T // 2
 ENTRIES = P * K
 LIST_COLUMNS = ENTRIES // 16
+
+CUTS = [[0, 512, 768, 1024], [0, 512, 1024], [0, 384, 1024], [0, 512, 1024]]
+PLACES = {(3, 1): 4096}
 
 FLOPS = 2 * D * M * G
 
@@ -35,12 +39,15 @@ def tile_attend_grid_bias_kernel(tc, xT, w, part, bias, offs, out):
     nc = tc.nc
     with ExitStack() as ctx:
         keep = ctx.enter_context(tc.tile_pool(name="keep", bufs=1))
+        arena = ctx.enter_context(tc.tile_pool(name="arena", bufs=1))
         banks = ctx.enter_context(tc.psum_pool(name="banks", bufs=1))
 
         def bank(name, on):
             return banks.tile([P, K, P], F32, name=name, tag=on)
 
         def sbuf(shape, dtype, name, on=None):
+            if isinstance(on, int):
+                return arena.tile(shape, dtype, align_bytes=64, name=name, tag=name, offset=on)
             return keep.tile(shape, dtype, align_bytes=64, name=name, tag=on or name)
 
         x_view = xT.rearrange("(s p t) c -> s p t c", p=P, t=PACK)
@@ -49,47 +56,53 @@ def tile_attend_grid_bias_kernel(tc, xT, w, part, bias, offs, out):
 
         pairs = [(s, u) for s in range(PASSES) for u in range(2)]
         table = [sbuf([P, T, 2], BF16, f"table{n}") for n in range(len(pairs))]
-        cuts = [[0, HALF, HALF + HALF // 2, T], [0, HALF, T], [0, HALF, T], [0, HALF, T]]
-        spans = [[slice(a, z) for a, z in zip(c, c[1:])] for c in cuts]
-        low_rows = {}
+        spans = [[slice(a, z) for a, z in zip(c, c[1:])] for c in CUTS]
+        rows = {}
         offsets = keep.tile([P, G * K // 16], U16, name="offsets")
         weights = keep.tile([P, BLOCKS, 8], F32, name="weights")
 
-        def load_low(n, h, on=None):
+        def load_rows(n, h):
             s, u = pairs[n]
             cols = spans[n][h]
-            low_rows[n, h] = sbuf([P, 2, cols.stop - cols.start], F32, f"low{n}_{h}", on)
-            nc.sync.dma_start(out=low_rows[n, h][:], in_=x_view[s, :, 2 * u : 2 * u + 2, cols])
+            rows[n, h] = sbuf([P, 2, cols.stop - cols.start], F32, f"rows{n}_{h}", PLACES.get((n, h)))
+            nc.sync.dma_start(out=rows[n, h][:], in_=x_view[s, :, 2 * u : 2 * u + 2, cols])
 
-        nc.scalar.dma_start(
-            out=weights[:, :, :K], in_=part[0:1, :].rearrange("o (b g j) -> (o g) b j", b=BLOCKS, j=K)
-        )
+        by_point = part[0:1, :].rearrange("o (b g j) -> (o g) b j", b=BLOCKS, j=K)
+        nc.scalar.dma_start(out=weights[:, :, :K], in_=by_point)
         w_whole = sbuf([P, PASSES, PACK, M], F32, "w_rows")
         bias_cols = sbuf([P, CHANNELS], F32, "bias_cols")
         for n in range(len(pairs)):
             for h in range(len(spans[n])):
-                load_low(n, h)
+                load_rows(n, h)
             if n == 0:
                 nc.sync.dma_start(offsets[:], offs)
         nc.sync.dma_start(out=w_whole[:], in_=w_view)
         nc.sync.dma_start(out=bias_cols[:], in_=bias.rearrange("(i m) o -> m (i o)", m=P))
 
         ident = keep.tile([P, P], F32, name="ident")
+        ones = sbuf([P, QUADRANT], F32, "ones")
+        column = sbuf([P, QUADRANT], F32, "column")
+        row = sbuf([P, QUADRANT], F32, "row")
+        nc.vector.memset(ones[:], 1.0)
         nc.vector.memset(ident[:], 0.0)
-        make_identity(nc, ident[:], nomemset=True)
+        nc.vector.tensor_tensor_scan(out=column[:], data0=ones[:], data1=ones[:], initial=0.0, op0=MULT, op1=ADD)
+        nc.vector.transpose(out=row[:], in_=column[:])
+        for q in range(0, P, QUADRANT):
+            own = slice(q, q + QUADRANT)
+            nc.vector.tensor_tensor(out=ident[own, own], in0=column[own, :], in1=row[own, :], op=EQUAL)
 
-        e_values = [sbuf([P, G, PACK], BF16, f"e_values{s}") for s in range(PASSES)]
+        e_values = {}
         e_codes = [sbuf([P, G], U32, f"e_codes{s}") for s in range(PASSES)]
         w_codes = sbuf([P, PASSES * M], U32, "w_codes")
-        sums = {(s, b): bank(f"sums{s}_{b}", f"sums{s}_{b}") for s in range(PASSES) for b in range(BLOCKS)}
+        sums = {}
         words = {}
         turned = {}
         w_scales = {}
         e_scales = {}
-        seen = {}
+        products = {}
 
         def cast(n, h, engine):
-            src = low_rows[n, h][:].rearrange("p e c -> p c e")
+            src = rows[n, h][:].rearrange("p e c -> p c e")
             if engine == "scalar":
                 nc.scalar.activation(out=table[n][:, spans[n][h], :], in_=src, func=COPY)
             else:
@@ -106,109 +119,140 @@ def tile_attend_grid_bias_kernel(tc, xT, w, part, bias, offs, out):
             into = bank(f"turned{n}_{b}_{corners[0]}", on)
             for j in corners:
                 nc.tensor.transpose(into[:, j, :], words[n, b][:, j // 2, :, j % 2].bitcast(F32), ident[:])
-                turned[n, b, j] = into
+                turned[n, b, j] = into[:, j, :]
+
+        def turn_both(s, b, h, on):
+            into = bank(f"turned_both{s}_{b}_{h}", on)
+            for u in range(2):
+                for i in range(2):
+                    nc.tensor.transpose(into[:, 2 * i + u, :], words[2 * s + u, b][:, h, :, i].bitcast(F32), ident[:])
+            return into
 
         def corner(n, b, j):
-            halves = turned[n, b, j][:, j, :].bitcast(BF16).rearrange("g (p e) -> g e p", e=2)
+            halves = turned[n, b, j].bitcast(BF16).rearrange("g (p e) -> g e p", e=2)
             return halves, weights[:, b, j : j + 1]
 
-        def add_up(n, b, weighted, count):
+        def add_up(n, b, terms):
             s, u = pairs[n]
-            slots = weighted if isinstance(weighted, list) else [weighted[:, j] for j in range(count)]
             for e in range(2):
-                for j in range(count):
+                for i, term in enumerate(terms):
                     nc.tensor.matmul(
-                        sums[s, b][:, 2 * u + e, :],
-                        slots[j][:, e, :],
-                        ident[:],
-                        start=(j == 0),
-                        stop=(j == count - 1),
-                        is_transpose=True,
+                        sums[s, b][:, 2 * u + e, :], term[:, e, :], ident[:],
+                        start=(i == 0), stop=(i == len(terms) - 1), is_transpose=True,
                     )
 
-        def weigh_four(n, b, on=None):
-            weighted = sbuf([P, K, 2, P], F32, f"weighted{n}_{b}", on)
-            for j in range(K):
+        def add_up_by_terms(n, b, terms):
+            s, u = pairs[n]
+            for i, term in enumerate(terms):
+                for e in range(2):
+                    nc.tensor.matmul(
+                        sums[s, b][:, 2 * u + e, :], term[:, e, :], ident[:],
+                        start=(i == 0 and e == 0), stop=(i == len(terms) - 1 and e == 1), is_transpose=True,
+                    )
+
+        def weigh(n, b, corners, engine, on=None):
+            weighted = sbuf([P, len(corners), 2, P], F32, f"weighted{n}_{b}_{corners[0]}", on)
+            for i, j in enumerate(corners):
                 halves, weight = corner(n, b, j)
-                nc.scalar.activation(out=weighted[:, j], in_=halves, func=COPY, scale=weight)
-            return weighted
+                if engine == "scalar":
+                    nc.scalar.activation(out=weighted[:, i], in_=halves, func=COPY, scale=weight)
+                else:
+                    nc.vector.tensor_scalar(out=weighted[:, i], in0=halves, scalar1=weight, scalar2=None, op0=MULT)
+            return [weighted[:, i] for i in range(len(corners))]
 
-        def weigh_two(n, b, h, on):
-            weighted = sbuf([P, 2, 2, P], F32, f"weighted{n}_{b}_{h}", on)
-            for i in range(2):
-                halves, weight = corner(n, b, 2 * h + i)
-                nc.scalar.activation(out=weighted[:, i], in_=halves, func=COPY, scale=weight)
-            return [weighted[:, i] for i in range(2)]
-
-        def add_pairs(n, b, weighted):
-            twos = sbuf([P, 2, 2, P], F32, f"twos{n}_{b}")
-            nc.gpsimd.tensor_tensor(out=twos[:], in0=weighted[:, 0:2], in1=weighted[:, 2:4], op=ADD)
-            add_up(n, b, twos, 2)
-
-        def weigh(n, b, on=None):
-            add_up(n, b, weigh_four(n, b, on), K)
-
-        def weigh_even(n, b, on=None, into=None):
-            even = sbuf([P, 2, 2, P], F32, f"even{n}_{b}", on) if into is None else into
-            for i in range(2):
-                halves, weight = corner(n, b, 2 * i)
-                nc.scalar.activation(out=even[:, i], in_=halves, func=COPY, scale=weight)
-            return even
-
-        def weigh_odd(n, b, even, on=None):
-            twos = sbuf([P, 2, 2, P], F32, f"twos{n}_{b}", on)
-            for i in range(2):
-                halves, weight = corner(n, b, 2 * i + 1)
+        def weigh_onto(n, b, corners, terms, on=None):
+            twos = sbuf([P, len(corners), 2, P], F32, f"twos{n}_{b}_{corners[0]}", on)
+            for i, j in enumerate(corners):
+                halves, weight = corner(n, b, j)
                 nc.vector.scalar_tensor_tensor(
-                    out=twos[:, i], in0=halves, scalar=weight, in1=even[:, i], op0=MULT, op1=ADD
+                    out=twos[:, i], in0=halves, scalar=weight, in1=terms[i], op0=MULT, op1=ADD
                 )
-            return twos
+            return [twos[:, i] for i in range(len(corners))]
 
-        def weigh_side_by_side(n, b):
-            weighted = sbuf([P, 3, 2, P], F32, f"weighted{n}_{b}")
-            third = sbuf([P, 2, P], F32, f"third{n}_{b}")
-            for j in range(2):
-                halves, weight = corner(n, b, j)
-                nc.scalar.activation(out=weighted[:, j], in_=halves, func=COPY, scale=weight)
-            halves, weight = corner(n, b, 2)
-            nc.vector.tensor_scalar(out=third[:], in0=halves, scalar1=weight, scalar2=None, op0=MULT)
-            halves, weight = corner(n, b, 3)
-            nc.vector.scalar_tensor_tensor(
-                out=weighted[:, 2], in0=halves, scalar=weight, in1=third[:], op0=MULT, op1=ADD
+        def weigh_both(s, b, both, on=None):
+            weighted = sbuf([P, K, 2, 2, P], F32, f"weighted_both{s}_{b}", on)
+            for j in range(K):
+                halves = both[j // 2][:, 2 * (j % 2) : 2 * (j % 2) + 2, :].bitcast(BF16).rearrange("g u (p e) -> g u e p", e=2)
+                nc.scalar.activation(out=weighted[:, j], in_=halves, func=COPY, scale=weights[:, b, j : j + 1])
+            return [[weighted[:, j, u] for j in range(K)] for u in range(2)]
+
+        def spread_weights(b, on, place):
+            into = bank(f"spread_bank{b}", on)
+            for j in range(K):
+                nc.tensor.transpose(into[:, j, :], weights[:, b, j : j + 1].to_broadcast([P, P]), ident[:])
+            spread = sbuf([P, 2, P, 2], F32, f"spread{b}", place)
+            nc.scalar.copy(out=spread[:], in_=into[:].rearrange("p (h j) g -> p h g j", h=2))
+            return spread
+
+        def weigh_unturned(n, b, spread, on=None):
+            weighted = sbuf([P, 2, ENTRIES], F32, f"unturned{n}_{b}", on)
+            halves = words[n, b][:].rearrange("p h g j -> p (h g j)").bitcast(BF16).rearrange("p (c e) -> p e c", e=2)
+            nc.gpsimd.tensor_tensor(
+                out=weighted[:], in0=halves,
+                in1=spread[:].rearrange("p h g j -> p (h g j)").unsqueeze(1).to_broadcast([P, 2, ENTRIES]), op=MULT,
             )
-            add_up(n, b, weighted, 3)
-            seen[n, b] = weighted
+            return weighted[:].rearrange("p e (h g j) -> p e h g j", h=2, j=2)
 
-        def weigh_alone(n, b, on):
-            even = sbuf([P, 2, 2, P], F32, f"even{n}_{b}", on)
-            for i in range(2):
-                halves, weight = corner(n, b, 2 * i)
-                nc.vector.tensor_scalar(out=even[:, i], in0=halves, scalar1=weight, scalar2=None, op0=MULT)
-            return weigh_odd(n, b, even)
+        def sum_unturned(n, b, weighted):
+            s, u = pairs[n]
+            twos = sbuf([P, 2, P, 2], F32, f"unturned_twos{n}_{b}")
+            nc.gpsimd.tensor_tensor(out=twos[:], in0=weighted[:, :, 0], in1=weighted[:, :, 1], op=ADD)
+            nc.gpsimd.tensor_tensor(
+                out=e_values[s, b][:, :, 2 * u : 2 * u + 2],
+                in0=twos[:, :, :, 0].rearrange("p e g -> p g e"), in1=twos[:, :, :, 1].rearrange("p e g -> p g e"), op=ADD,
+            )
 
-        def round_e(s, b):
-            points = slice(b * P, (b + 1) * P)
+        def add_turning(n, weighted, into):
+            u = n % 2
+            for e in range(2):
+                for j in range(K):
+                    nc.tensor.matmul(
+                        into[:, 2 * u + e, :], weighted[:, e, j // 2, :, j % 2], ident[:],
+                        start=(j == 0), stop=(j == K - 1), is_transpose=True,
+                    )
+
+        def round_by_points(into, u, on):
+            rounded = sbuf([P, P, 2], BF16, f"rounded{u}", on)
             nc.scalar.activation(
-                out=e_values[s][:, points, :], in_=sums[s, b][:].rearrange("p t g -> p g t"), func=COPY
+                out=rounded[:], in_=into[:, 2 * u : 2 * u + 2, :].rearrange("g e p -> g p e"), func=COPY
+            )
+            return rounded
+
+        def turn_back(rounded, on):
+            back = bank("back", on)
+            for u in range(2):
+                nc.tensor.transpose(back[:, u, :], rounded[u][:].rearrange("g p e -> g (p e)").bitcast(F32), ident[:])
+            return back
+
+        def copy_back(s, b, back):
+            nc.scalar.copy(
+                out=e_values[s, b][:].rearrange("p g t -> p (g t)").bitcast(F32).rearrange("p (g u) -> p g u", u=2),
+                in_=back[:, 0:2, :].rearrange("p u g -> p g u"),
             )
 
-        def quantize_e(s, points, on=None):
-            if s not in e_scales:
-                e_scales[s] = sbuf([P, G], U8, f"e_scales{s}", on)
+        def round_e(s, b, engine="scalar", places=slice(0, PACK)):
+            src = sums[s, b][:, places, :].rearrange("p t g -> p g t")
+            if engine == "scalar":
+                nc.scalar.activation(out=e_values[s, b][:, :, places], in_=src, func=COPY)
+            else:
+                nc.vector.tensor_copy(out=e_values[s, b][:, :, places], in_=src)
+
+        def quantize_e(s, b, on=None):
+            e_scales[s, b] = sbuf([P, P], U8, f"e_scales{s}_{b}", on)
             nc.vector.quantize_mx(
-                out=e_codes[s][:, points].bitcast(FP8X4),
-                scales=e_scales[s][:, points],
-                in_=e_values[s][:, points, :].rearrange("p g t -> p (g t)"),
+                out=e_codes[s][:, b * P : (b + 1) * P].bitcast(FP8X4),
+                scales=e_scales[s, b][:],
+                in_=e_values[s, b][:].rearrange("p g t -> p (g t)"),
             )
 
-        def round_w_whole(on):
+        def round_w(on=None):
             w_values = sbuf([P, PASSES, M, PACK], BF16, "w_values", on)
             nc.gpsimd.tensor_scalar(
                 out=w_values[:], in0=w_whole[:].rearrange("p s t m -> p s m t"), scalar1=1.0, scalar2=0.0, op0=MULT, op1=ADD
             )
             return w_values
 
-        def quantize_w_whole(w_values, on):
+        def quantize_w(w_values, on):
             scales = sbuf([P, PASSES * M], U8, "w_scales", on)
             for s in range(PASSES):
                 w_scales[s] = scales[:, s * M : (s + 1) * M]
@@ -221,11 +265,11 @@ def tile_attend_grid_bias_kernel(tc, xT, w, part, bias, offs, out):
             for i in range(CHANNELS):
                 channels = slice(s * M + i * P, s * M + (i + 1) * P)
                 nc.tensor.matmul_mx(
-                    out=products[b][i][:, 0, :],
+                    out=products[b, i][:, 0, :],
                     lhsT=w_codes[:, channels].bitcast(FP8X4),
                     lhsT_scale=w_scales[s][:, i * P : (i + 1) * P],
                     rhs=e_codes[s][:, points].bitcast(FP8X4),
-                    rhs_scale=e_scales[s][:, points],
+                    rhs_scale=e_scales[s, b][:],
                     start=(s == 0),
                     stop=(s == PASSES - 1),
                 )
@@ -233,65 +277,72 @@ def tile_attend_grid_bias_kernel(tc, xT, w, part, bias, offs, out):
         def finish(b, on=None):
             points = slice(b * P, (b + 1) * P)
             result = sbuf([P, CHANNELS, P], F32, f"result{b}", on)
-            nc.scalar.activation(out=result[:, 0], in_=products[b][0][:, 0, :], func=IDENTITY, bias=bias_cols[:, 0:1])
+            nc.scalar.activation(out=result[:, 0], in_=products[b, 0][:, 0, :], func=IDENTITY, bias=bias_cols[:, 0:1])
             nc.vector.tensor_scalar(
-                out=result[:, 1], in0=products[b][1][:, 0, :], scalar1=bias_cols[:, 1:2], scalar2=None, op0=ADD
+                out=result[:, 1], in0=products[b, 1][:, 0, :], scalar1=bias_cols[:, 1:2], scalar2=None, op0=ADD
             )
             nc.sync.dma_start(out=out_view[:, :, points], in_=result[:])
 
-        for h in range(len(spans[0])):
+        spread = spread_weights(1, "sums1_1", None)
+        for s in range(PASSES):
+            for b in range(BLOCKS):
+                sums[s, b] = bank(f"sums{s}_{b}", f"sums{s}_{b}")
+        e_values[0, 1] = sbuf([P, P, PACK], BF16, "e_values0_1")
+        for h in range(3):
             cast(0, h, "vector")
         gather(0, 0)
         gather(0, 1)
         cast(1, 0, "scalar")
-        cast(1, 1, "vector")
+        cast(1, 1, "scalar")
         cast(2, 0, "vector")
         gather(1, 0)
         gather(1, 1)
         turn(0, 0, "a", (0, 1))
         turn(0, 0, "c", (2, 3))
-        turn(0, 1, "b", (0, 1))
-        turn(0, 1, "d", (2, 3))
-        weighted = weigh_four(0, 0, on="low1_0")
+        terms = weigh(0, 0, range(K), "scalar", "rows1_1")
         turn(1, 0, "a")
-        add_up(0, 0, weighted, K)
-        weighted = weigh_four(0, 1)
+        add_up_by_terms(0, 0, terms)
         turn(1, 1, "b")
-        add_up(0, 1, weighted, K)
         cast(2, 1, "scalar")
         gather(2, 0)
         gather(2, 1)
         turn(2, 0, "c")
         turn(2, 1, "d")
-        for h in range(len(spans[3])):
-            cast(3, h, "scalar")
+        cast(3, 0, "scalar")
+        cast(3, 1, "scalar")
         gather(3, 0)
         gather(3, 1)
-        w_values = round_w_whole(None)
-        weighted = weigh_four(1, 0, on="low3_0")
+        sum_unturned(0, 1, weigh_unturned(0, 1, spread, "rows2_0"))
+        w_values = round_w()
+        terms = weigh(1, 0, range(K), "scalar", 7680)
         turn(3, 0, "a")
-        add_up(1, 0, weighted, K)
-        weighted = weigh_four(1, 1, on="low3_1")
+        add_up_by_terms(1, 0, terms)
+        terms = weigh(1, 1, range(K), "scalar", 512)
         turn(3, 1, "b")
-        add_up(1, 1, weighted, K)
-        even_20 = weigh_even(2, 0)
-        even_21 = weigh_even(2, 1)
-        even_30 = weigh_even(3, 0)
-        add_up(2, 0, weigh_odd(2, 0, even_20), 2)
-        add_up(2, 1, weigh_odd(2, 1, even_21), 2)
-        add_up(3, 0, weigh_odd(3, 0, even_30), 2)
-        add_up(3, 1, weigh_odd(3, 1, weigh_even(3, 1)), 2)
+        add_up_by_terms(1, 1, terms)
+        terms = weigh_onto(2, 0, (1, 3), weigh(2, 0, (0, 2), "vector", "words3_0"))
+        add_up_by_terms(2, 0, terms)
+        even_21 = weigh(2, 1, (0, 2), "scalar", 4608)
+        even_30 = weigh(3, 0, (0, 2), "scalar")
+        terms = weigh(3, 1, range(K), "scalar")
+        round_e(0, 1, "scalar", slice(2, 4))
+        add_up_by_terms(2, 1, weigh_onto(2, 1, (1, 3), even_21))
+        add_up_by_terms(3, 0, weigh_onto(3, 0, (1, 3), even_30))
+        add_up_by_terms(3, 1, terms)
+        e_values[0, 0] = sbuf([P, P, PACK], BF16, "e_values0_0", "weighted3_0_0")
+        e_values[1, 0] = sbuf([P, P, PACK], BF16, "e_values1_0")
+        e_values[1, 1] = sbuf([P, P, PACK], BF16, "e_values1_1")
         round_e(0, 0)
-        round_e(0, 1)
+        quantize_w(w_values, 4608)
+        quantize_e(0, 1, 5632)
         round_e(1, 0)
         round_e(1, 1)
-        quantize_w_whole(w_values, "even3_0")
-        quantize_e(0, slice(0, G), "even3_1")
-        quantize_e(1, slice(0, P))
-        quantize_e(1, slice(P, G))
-        products = [[bank(f"products{b}_{i}", on) for i, on in enumerate(ons)] for b, ons in enumerate((("sums0_0", "sums0_1"), ("c", "d")))]
-        for s in range(PASSES):
-            for b in range(BLOCKS):
-                multiply(s, b)
-        finish(0, "e_values1")
+        quantize_e(0, 0)
+        quantize_e(1, 0)
+        quantize_e(1, 1)
+        for (b, i), on in {(0, 0): "sums0_0", (0, 1): "a", (1, 0): "sums0_1", (1, 1): "d"}.items():
+            products[b, i] = bank(f"products{b}_{i}", on)
+        for s, b in ((0, 1), (0, 0), (1, 0), (1, 1)):
+            multiply(s, b)
+        finish(0, "e_values1_1")
         finish(1)

@@ -29,8 +29,8 @@ HALF = T // 2
 ENTRIES = P * K
 LIST_COLUMNS = ENTRIES // 16
 
-CUTS = [[0, 512, 768, 1024], [0, 512, 1024], [0, 384, 1024], [0, 512, 1024]]
-PLACES = {(3, 1): 4096}
+CUTS = [[0, 512, 768, 1024], [0, 512, 1024], [0, 512, 1024], [0, 512, 1024]]
+PLACES = {(3, 1): 8192}
 
 FLOPS = 2 * D * M * G
 
@@ -202,6 +202,15 @@ def tile_attend_grid_bias_kernel(tc, xT, w, part, bias, offs, out):
                 in0=twos[:, :, :, 0].rearrange("p e g -> p g e"), in1=twos[:, :, :, 1].rearrange("p e g -> p g e"), op=ADD,
             )
 
+        def add_halves(n, weighted, twos):
+            u = n % 2
+            nc.gpsimd.tensor_tensor(
+                out=twos[:, :, 2 * u : 2 * u + 2, :],
+                in0=weighted[:, :, 0].rearrange("p e g j -> p g e j"),
+                in1=weighted[:, :, 1].rearrange("p e g j -> p g e j"),
+                op=ADD,
+            )
+
         def add_turning(n, weighted, into):
             u = n % 2
             for e in range(2):
@@ -245,8 +254,8 @@ def tile_attend_grid_bias_kernel(tc, xT, w, part, bias, offs, out):
                 in_=e_values[s, b][:].rearrange("p g t -> p (g t)"),
             )
 
-        def round_w(on=None):
-            w_values = sbuf([P, PASSES, M, PACK], BF16, "w_values", on)
+        def round_w():
+            w_values = sbuf([P, PASSES, M, PACK], BF16, "w_values")
             nc.gpsimd.tensor_scalar(
                 out=w_values[:], in0=w_whole[:].rearrange("p s t m -> p s m t"), scalar1=1.0, scalar2=0.0, op0=MULT, op1=ADD
             )
@@ -283,66 +292,54 @@ def tile_attend_grid_bias_kernel(tc, xT, w, part, bias, offs, out):
             )
             nc.sync.dma_start(out=out_view[:, :, points], in_=result[:])
 
-        spread = spread_weights(1, "sums1_1", None)
-        for s in range(PASSES):
-            for b in range(BLOCKS):
-                sums[s, b] = bank(f"sums{s}_{b}", f"sums{s}_{b}")
-        e_values[0, 1] = sbuf([P, P, PACK], BF16, "e_values0_1")
+        spread = spread_weights(0, "sums1_1", None)
+        for s, b in ((0, 1), (1, 0), (1, 1)):
+            sums[s, b] = bank(f"sums{s}_{b}", f"sums{s}_{b}")
+        twos = sbuf([P, P, PACK, 2], F32, "unturned_twos")
         for h in range(3):
             cast(0, h, "vector")
         gather(0, 0)
         gather(0, 1)
-        cast(1, 0, "scalar")
-        cast(1, 1, "scalar")
-        cast(2, 0, "vector")
-        gather(1, 0)
-        gather(1, 1)
-        turn(0, 0, "a", (0, 1))
-        turn(0, 0, "c", (2, 3))
-        terms = weigh(0, 0, range(K), "scalar", "rows1_1")
-        turn(1, 0, "a")
-        add_up_by_terms(0, 0, terms)
-        turn(1, 1, "b")
-        cast(2, 1, "scalar")
-        gather(2, 0)
-        gather(2, 1)
+        for n in range(1, 4):
+            cast(n, 0, "scalar")
+            cast(n, 1, "scalar")
+            gather(n, 0)
+            gather(n, 1)
+        for n in range(2):
+            add_halves(n, weigh_unturned(n, 0, spread), twos)
+        w_values = round_w()
+        both = [turn_both(0, 1, h, on) for h, on in enumerate(("a", "b"))]
         turn(2, 0, "c")
         turn(2, 1, "d")
-        cast(3, 0, "scalar")
-        cast(3, 1, "scalar")
-        gather(3, 0)
-        gather(3, 1)
-        sum_unturned(0, 1, weigh_unturned(0, 1, spread, "rows2_0"))
-        w_values = round_w()
-        terms = weigh(1, 0, range(K), "scalar", 7680)
+        terms = weigh_both(0, 1, both, 512)
         turn(3, 0, "a")
-        add_up_by_terms(1, 0, terms)
-        terms = weigh(1, 1, range(K), "scalar", 512)
         turn(3, 1, "b")
-        add_up_by_terms(1, 1, terms)
-        terms = weigh_onto(2, 0, (1, 3), weigh(2, 0, (0, 2), "vector", "words3_0"))
-        add_up_by_terms(2, 0, terms)
-        even_21 = weigh(2, 1, (0, 2), "scalar", 4608)
-        even_30 = weigh(3, 0, (0, 2), "scalar")
+        add_up_by_terms(0, 1, terms[0])
+        add_up_by_terms(1, 1, terms[1])
+        even_20 = weigh(2, 0, (0, 2), "scalar", 8704)
+        even_21 = weigh(2, 1, (0, 2), "scalar", 10752)
+        even_30 = weigh(3, 0, (0, 2), "scalar", 16384)
         terms = weigh(3, 1, range(K), "scalar")
-        round_e(0, 1, "scalar", slice(2, 4))
+        add_up_by_terms(2, 0, weigh_onto(2, 0, (1, 3), even_20))
         add_up_by_terms(2, 1, weigh_onto(2, 1, (1, 3), even_21))
         add_up_by_terms(3, 0, weigh_onto(3, 0, (1, 3), even_30))
         add_up_by_terms(3, 1, terms)
-        e_values[0, 0] = sbuf([P, P, PACK], BF16, "e_values0_0", "weighted3_0_0")
+        e_values[0, 0] = sbuf([P, P, PACK], BF16, "e_values0_0", 16384)
+        nc.vector.tensor_tensor(out=e_values[0, 0][:], in0=twos[:, :, :, 0], in1=twos[:, :, :, 1], op=ADD)
+        e_values[0, 1] = sbuf([P, P, PACK], BF16, "e_values0_1", "words3_1")
         e_values[1, 0] = sbuf([P, P, PACK], BF16, "e_values1_0")
         e_values[1, 1] = sbuf([P, P, PACK], BF16, "e_values1_1")
-        round_e(0, 0)
-        quantize_w(w_values, 4608)
-        quantize_e(0, 1, 5632)
+        round_e(0, 1)
         round_e(1, 0)
         round_e(1, 1)
+        quantize_w(w_values, 17408)
         quantize_e(0, 0)
+        quantize_e(0, 1)
         quantize_e(1, 0)
         quantize_e(1, 1)
-        for (b, i), on in {(0, 0): "sums0_0", (0, 1): "a", (1, 0): "sums0_1", (1, 1): "d"}.items():
+        for (b, i), on in {(0, 0): "e", (0, 1): "c", (1, 0): "sums0_1", (1, 1): "d"}.items():
             products[b, i] = bank(f"products{b}_{i}", on)
-        for s, b in ((0, 1), (0, 0), (1, 0), (1, 1)):
+        for s, b in ((0, 0), (0, 1), (1, 0), (1, 1)):
             multiply(s, b)
         finish(0, "e_values1_1")
         finish(1)

@@ -29,7 +29,7 @@ HALF = T // 2
 ENTRIES = P * K
 LIST_COLUMNS = ENTRIES // 16
 
-CUTS = [[0, 512, 768, 1024], [0, 512, 1024], [0, 512, 1024], [0, 512, 1024]]
+CUTS = [[0, 512, 1024], [0, 512, 1024], [0, 512, 1024], [0, 512, 1024]]
 PLACES = {(3, 1): 8192}
 
 FLOPS = 2 * D * M * G
@@ -58,17 +58,22 @@ def tile_attend_grid_bias_kernel(tc, xT, w, part, bias, offs, out):
         table = [sbuf([P, T, 2], BF16, f"table{n}") for n in range(len(pairs))]
         spans = [[slice(a, z) for a, z in zip(c, c[1:])] for c in CUTS]
         rows = {}
+        first_rows = sbuf([P, 2 * T], F32, "first_rows")
         offsets = keep.tile([P, G * K // 16], U16, name="offsets")
         weights = keep.tile([P, BLOCKS, 8], F32, name="weights")
 
         def load_rows(n, h):
             s, u = pairs[n]
             cols = spans[n][h]
+            if n == 0:
+                run = slice(0, T + HALF) if h == 0 else slice(T + HALF, 2 * T)
+                nc.sync.dma_start(out=first_rows[:, run], in_=x_view[0, :, 0:2, :].rearrange("p e c -> p (e c)")[:, run])
+                return
             rows[n, h] = sbuf([P, 2, cols.stop - cols.start], F32, f"rows{n}_{h}", PLACES.get((n, h)))
             nc.sync.dma_start(out=rows[n, h][:], in_=x_view[s, :, 2 * u : 2 * u + 2, cols])
 
         by_point = part[0:1, :].rearrange("o (b g j) -> (o g) b j", b=BLOCKS, j=K)
-        nc.scalar.dma_start(out=weights[:, :, :K], in_=by_point)
+        nc.scalar.dma_start(out=weights[:, 0, :K], in_=by_point[:, 0])
         w_whole = sbuf([P, PASSES, PACK, M], F32, "w_rows")
         bias_cols = sbuf([P, CHANNELS], F32, "bias_cols")
         for n in range(len(pairs)):
@@ -76,6 +81,7 @@ def tile_attend_grid_bias_kernel(tc, xT, w, part, bias, offs, out):
                 load_rows(n, h)
             if n == 0:
                 nc.sync.dma_start(offsets[:], offs)
+        nc.sync.dma_start(out=weights[:, 1, :K], in_=by_point[:, 1])
         nc.sync.dma_start(out=w_whole[:], in_=w_view)
         nc.sync.dma_start(out=bias_cols[:], in_=bias.rearrange("(i m) o -> m (i o)", m=P))
 
@@ -102,7 +108,10 @@ def tile_attend_grid_bias_kernel(tc, xT, w, part, bias, offs, out):
         products = {}
 
         def cast(n, h, engine):
-            src = rows[n, h][:].rearrange("p e c -> p c e")
+            if n == 0:
+                src = first_rows[:].rearrange("p (e c) -> p c e", e=2)[:, spans[n][h], :]
+            else:
+                src = rows[n, h][:].rearrange("p e c -> p c e")
             if engine == "scalar":
                 nc.scalar.activation(out=table[n][:, spans[n][h], :], in_=src, func=COPY)
             else:
@@ -296,7 +305,7 @@ def tile_attend_grid_bias_kernel(tc, xT, w, part, bias, offs, out):
         for s, b in ((0, 1), (1, 0), (1, 1)):
             sums[s, b] = bank(f"sums{s}_{b}", f"sums{s}_{b}")
         twos = sbuf([P, P, PACK, 2], F32, "unturned_twos")
-        for h in range(3):
+        for h in range(2):
             cast(0, h, "vector")
         gather(0, 0)
         gather(0, 1)

@@ -47,8 +47,8 @@ def tile_attend_grid_bias_kernel(tc, xT, w, part, bias, offs, out):
 
         def sbuf(shape, dtype, name, on=None):
             if isinstance(on, int):
-                return arena.tile(shape, dtype, align_bytes=64, name=name, tag=name, offset=on)
-            return keep.tile(shape, dtype, align_bytes=64, name=name, tag=on or name)
+                return arena.tile(shape, dtype, align_bytes=256, name=name, tag=name, offset=on)
+            return keep.tile(shape, dtype, align_bytes=256, name=name, tag=on or name)
 
         x_view = xT.rearrange("(s p t) c -> s p t c", p=P, t=PACK)
         w_view = w.rearrange("(s p t) m -> p s t m", p=P, t=PACK)

@@ -295,11 +295,15 @@ def tile_attend_grid_bias_kernel(tc, xT, w, part, bias, offs, out):
         def finish(b, on=None):
             points = slice(b * P, (b + 1) * P)
             result = sbuf([P, CHANNELS, P], F32, f"result{b}", on)
-            nc.scalar.activation(out=result[:, 0], in_=products[b, 0][:, 0, :], func=IDENTITY, bias=bias_cols[:, 0:1])
             nc.vector.tensor_scalar(
-                out=result[:, 1], in0=products[b, 1][:, 0, :], scalar1=bias_cols[:, 1:2], scalar2=None, op0=ADD
+                out=result[:, 0], in0=products[b, 0][:, 0, :], scalar1=bias_cols[:, 0:1], scalar2=None, op0=ADD
             )
-            nc.sync.dma_start(out=out_view[:, :, points], in_=result[:])
+            nc.scalar.activation(out=result[:, 1], in_=products[b, 1][:, 0, :], func=IDENTITY, bias=bias_cols[:, 1:2])
+            if b == 0:
+                nc.sync.dma_start(out=out_view[:, :, points], in_=result[:])
+            else:
+                nc.sync.dma_start(out=out_view[:, 0, points], in_=result[:, 0])
+                nc.scalar.dma_start(out=out_view[:, 1, points], in_=result[:, 1])
 
         spread = spread_weights(0, "sums1_1", None)
         for s, b in ((0, 1), (1, 0), (1, 1)):

@@ -30,7 +30,7 @@ ENTRIES = P * K
 LIST_COLUMNS = ENTRIES // 16
 
 CUTS = [[0, 512, 1024], [0, 512, 1024], [0, 512, 1024], [0, 512, 1024]]
-PLACES = {(3, 1): 8192}
+PLACES = {}
 
 FLOPS = 2 * D * M * G
 
@@ -55,12 +55,14 @@ def tile_attend_grid_bias_kernel(tc, xT, w, part, bias, offs, out):
         out_view = out.rearrange("(i m) g -> m i g", m=P)
 
         pairs = [(s, u) for s in range(PASSES) for u in range(2)]
-        table = [sbuf([P, T, 2], BF16, f"table{n}") for n in range(len(pairs))]
+        table = [sbuf([P, T, 2], BF16, "table0")] + [sbuf([P, 2, T], F32, f"table{n}") for n in range(1, len(pairs))]
         spans = [[slice(a, z) for a, z in zip(c, c[1:])] for c in CUTS]
         rows = {}
         first_rows = sbuf([P, 2 * T], F32, "first_rows")
         offsets = keep.tile([P, G * K // 16], U16, name="offsets")
         weights = keep.tile([P, BLOCKS, 8], F32, name="weights")
+
+        early_weights = keep.tile([P, 8], F32, name="early_weights")
 
         def load_rows(n, h):
             s, u = pairs[n]
@@ -69,11 +71,10 @@ def tile_attend_grid_bias_kernel(tc, xT, w, part, bias, offs, out):
                 run = slice(0, T + HALF) if h == 0 else slice(T + HALF, 2 * T)
                 nc.sync.dma_start(out=first_rows[:, run], in_=x_view[0, :, 0:2, :].rearrange("p e c -> p (e c)")[:, run])
                 return
-            rows[n, h] = sbuf([P, 2, cols.stop - cols.start], F32, f"rows{n}_{h}", PLACES.get((n, h)))
-            nc.sync.dma_start(out=rows[n, h][:], in_=x_view[s, :, 2 * u : 2 * u + 2, cols])
+            nc.sync.dma_start(out=table[n][:, :, cols], in_=x_view[s, :, 2 * u : 2 * u + 2, cols])
 
         by_point = part[0:1, :].rearrange("o (b g j) -> (o g) b j", b=BLOCKS, j=K)
-        nc.scalar.dma_start(out=weights[:, 0, :K], in_=by_point[:, 0])
+        nc.scalar.dma_start(out=early_weights[:, :K], in_=by_point[:, 0])
         w_whole = sbuf([P, PASSES, PACK, M], F32, "w_rows")
         bias_cols = sbuf([P, CHANNELS], F32, "bias_cols")
         for n in range(len(pairs)):
@@ -81,7 +82,7 @@ def tile_attend_grid_bias_kernel(tc, xT, w, part, bias, offs, out):
                 load_rows(n, h)
             if n == 0:
                 nc.sync.dma_start(offsets[:], offs)
-        nc.sync.dma_start(out=weights[:, 1, :K], in_=by_point[:, 1])
+        nc.sync.dma_start(out=weights[:, :, :K], in_=by_point)
         nc.sync.dma_start(out=w_whole[:], in_=w_view)
         nc.sync.dma_start(out=bias_cols[:], in_=bias.rearrange("(i m) o -> m (i o)", m=P))
 
@@ -107,6 +108,10 @@ def tile_attend_grid_bias_kernel(tc, xT, w, part, bias, offs, out):
         e_scales = {}
         products = {}
 
+        def cast_low(n, h):
+            low = table[n][:, 1, :].bitcast(BF16).rearrange("p (c e) -> p c e", e=2)[:, spans[n][h], 0]
+            nc.scalar.activation(out=low, in_=table[n][:, 0, spans[n][h]], func=COPY)
+
         def cast(n, h, engine):
             if n == 0:
                 src = first_rows[:].rearrange("p (e c) -> p c e", e=2)[:, spans[n][h], :]
@@ -121,7 +126,7 @@ def tile_attend_grid_bias_kernel(tc, xT, w, part, bias, offs, out):
             words[n, b] = sbuf([P, 2, P, 2], U32, f"words{n}_{b}", on)
             nc.vector.tensor_copy(
                 out=words[n, b][:].rearrange("p h g j -> p g h j"),
-                in_=table[n][:].rearrange("p c e -> p (c e)").bitcast(U32).indirect(offsets[:, b * LIST_COLUMNS : (b + 1) * LIST_COLUMNS]),
+                in_=(table[n][:, 1, :] if n else table[n][:].rearrange("p c e -> p (c e)")).bitcast(U32).indirect(offsets[:, b * LIST_COLUMNS : (b + 1) * LIST_COLUMNS]),
             )
 
         def turn(n, b, on, corners=range(K)):
@@ -188,7 +193,7 @@ def tile_attend_grid_bias_kernel(tc, xT, w, part, bias, offs, out):
         def spread_weights(b, on, place):
             into = bank(f"spread_bank{b}", on)
             for j in range(K):
-                nc.tensor.transpose(into[:, j, :], weights[:, b, j : j + 1].to_broadcast([P, P]), ident[:])
+                nc.tensor.transpose(into[:, j, :], early_weights[:, j : j + 1].to_broadcast([P, P]), ident[:])
             spread = sbuf([P, 2, P, 2], F32, f"spread{b}", place)
             nc.scalar.copy(out=spread[:], in_=into[:].rearrange("p (h j) g -> p h g j", h=2))
             return spread
@@ -314,8 +319,8 @@ def tile_attend_grid_bias_kernel(tc, xT, w, part, bias, offs, out):
         gather(0, 0)
         gather(0, 1)
         for n in range(1, 4):
-            cast(n, 0, "scalar")
-            cast(n, 1, "scalar")
+            cast_low(n, 0)
+            cast_low(n, 1)
             gather(n, 0)
             gather(n, 1)
         for n in range(2):

@@ -123,7 +123,11 @@ def tile_attend_grid_bias_kernel(tc, xT, w, part, bias, offs, out):
                 nc.vector.tensor_copy(out=table[n][:, spans[n][h], :], in_=src)
 
         def gather(n, b, on=None):
-            words[n, b] = sbuf([P, 2, P, 2], U32, f"words{n}_{b}", on)
+            if n == 3:
+                by_corner = sbuf([P, 2, 2, P], U32, f"words{n}_{b}", on)
+                words[n, b] = by_corner[:].rearrange("p h j g -> p h g j")
+            else:
+                words[n, b] = sbuf([P, 2, P, 2], U32, f"words{n}_{b}", on)
             nc.vector.tensor_copy(
                 out=words[n, b][:].rearrange("p h g j -> p g h j"),
                 in_=(table[n][:, 1, :] if n else table[n][:].rearrange("p c e -> p (c e)")).bitcast(U32).indirect(offsets[:, b * LIST_COLUMNS : (b + 1) * LIST_COLUMNS]),

from contextlib import ExitStack

import concourse.mybir as mybir

F32 = mybir.dt.float32
BF16 = mybir.dt.bfloat16
U32 = mybir.dt.uint32
U16 = mybir.dt.uint16
U8 = mybir.dt.uint8
FP8X4 = mybir.dt.float8_e4m3fn_x4
COPY = mybir.ActivationFunctionType.Copy
IDENTITY = mybir.ActivationFunctionType.Identity
EQUAL = mybir.AluOpType.is_equal
ADD = mybir.AluOpType.add
MULT = mybir.AluOpType.mult

P = 128
D = 1024
T = 1024
M = 256
G = 256
K = 4
PACK = 4
PASSES = D // (P * PACK)
BLOCKS = G // P
CHANNELS = M // P
QUADRANT = 32
HALF = T // 2
ENTRIES = P * K
LIST_COLUMNS = ENTRIES // 16

CUTS = [[0, 512, 1024], [0, 512, 1024], [0, 512, 1024], [0, 512, 1024]]
PLACES = {}

FLOPS = 2 * D * M * G


def tile_attend_grid_bias_kernel(tc, xT, w, part, bias, offs, out):
    nc = tc.nc
    with ExitStack() as ctx:
        keep = ctx.enter_context(tc.tile_pool(name="keep", bufs=1))
        arena = ctx.enter_context(tc.tile_pool(name="arena", bufs=1))
        banks = ctx.enter_context(tc.psum_pool(name="banks", bufs=1))

        def bank(name, on):
            return banks.tile([P, K, P], F32, name=name, tag=on)

        def sbuf(shape, dtype, name, on=None):
            if isinstance(on, int):
                return arena.tile(shape, dtype, align_bytes=256, name=name, tag=name, offset=on)
            return keep.tile(shape, dtype, align_bytes=256, name=name, tag=on or name)

        x_view = xT.rearrange("(s p t) c -> s p t c", p=P, t=PACK)
        w_view = w.rearrange("(s p t) m -> p s t m", p=P, t=PACK)
        out_view = out.rearrange("(i m) g -> m i g", m=P)

        pairs = [(s, u) for s in range(PASSES) for u in range(2)]
        table = [sbuf([P, T, 2], BF16, "table0")] + [sbuf([P, 2, T], F32, f"table{n}") for n in range(1, len(pairs))]
        spans = [[slice(a, z) for a, z in zip(c, c[1:])] for c in CUTS]
        rows = {}
        first_rows = sbuf([P, 2 * T], F32, "first_rows")
        offsets = keep.tile([P, G * K // 16], U16, name="offsets")
        weights = keep.tile([P, BLOCKS, 8], F32, name="weights")

        early_weights = keep.tile([P, 8], F32, name="early_weights")

        def load_rows(n, h):
            s, u = pairs[n]
            cols = spans[n][h]
            if n == 0:
                run = slice(0, T + HALF) if h == 0 else slice(T + HALF, 2 * T)
                nc.sync.dma_start(out=first_rows[:, run], in_=x_view[0, :, 0:2, :].rearrange("p e c -> p (e c)")[:, run])
                return
            nc.sync.dma_start(out=table[n][:, :, cols], in_=x_view[s, :, 2 * u : 2 * u + 2, cols])

        by_point = part[0:1, :].rearrange("o (b g j) -> (o g) b j", b=BLOCKS, j=K)
        nc.scalar.dma_start(out=early_weights[:, :K], in_=by_point[:, 0])
        w_whole = sbuf([P, PASSES, PACK, M], F32, "w_rows")
        bias_cols = sbuf([P, CHANNELS], F32, "bias_cols")
        for n in range(len(pairs)):
            for h in range(len(spans[n])):
                load_rows(n, h)
            if n == 0:
                nc.sync.dma_start(offsets[:], offs)
        nc.sync.dma_start(out=weights[:, :, :K], in_=by_point)
        nc.sync.dma_start(out=w_whole[:], in_=w_view)
        nc.sync.dma_start(out=bias_cols[:], in_=bias.rearrange("(i m) o -> m (i o)", m=P))

        ident = keep.tile([P, P], F32, name="ident")
        ones = sbuf([P, QUADRANT], F32, "ones")
        column = sbuf([P, QUADRANT], F32, "column")
        row = sbuf([P, QUADRANT], F32, "row")
        nc.vector.memset(ones[:], 1.0)
        nc.vector.memset(ident[:], 0.0)
        nc.vector.tensor_tensor_scan(out=column[:], data0=ones[:], data1=ones[:], initial=0.0, op0=MULT, op1=ADD)
        nc.vector.transpose(out=row[:], in_=column[:])
        for q in range(0, P, QUADRANT):
            own = slice(q, q + QUADRANT)
            nc.vector.tensor_tensor(out=ident[own, own], in0=column[own, :], in1=row[own, :], op=EQUAL)

        e_values = {}
        e_codes = [sbuf([P, G], U32, f"e_codes{s}") for s in range(PASSES)]
        w_codes = sbuf([P, PASSES * M], U32, "w_codes")
        sums = {}
        words = {}
        turned = {}
        w_scales = {}
        e_scales = {}
        products = {}

        def cast_low(n, h):
            low = table[n][:, 1, :].bitcast(BF16).rearrange("p (c e) -> p c e", e=2)[:, spans[n][h], 0]
            nc.scalar.activation(out=low, in_=table[n][:, 0, spans[n][h]], func=COPY)

        def cast(n, h, engine):
            if n == 0:
                src = first_rows[:].rearrange("p (e c) -> p c e", e=2)[:, spans[n][h], :]
            else:
                src = rows[n, h][:].rearrange("p e c -> p c e")
            if engine == "scalar":
                nc.scalar.activation(out=table[n][:, spans[n][h], :], in_=src, func=COPY)
            else:
                nc.vector.tensor_copy(out=table[n][:, spans[n][h], :], in_=src)

        def gather(n, b, on=None):
            if n == 3:
                by_corner = sbuf([P, 2, 2, P], U32, f"words{n}_{b}", on)
                words[n, b] = by_corner[:].rearrange("p h j g -> p h g j")
            else:
                words[n, b] = sbuf([P, 2, P, 2], U32, f"words{n}_{b}", on)
            nc.vector.tensor_copy(
                out=words[n, b][:].rearrange("p h g j -> p g h j"),
                in_=(table[n][:, 1, :] if n else table[n][:].rearrange("p c e -> p (c e)")).bitcast(U32).indirect(offsets[:, b * LIST_COLUMNS : (b + 1) * LIST_COLUMNS]),
            )

        def turn(n, b, on, corners=range(K)):
            into = bank(f"turned{n}_{b}_{corners[0]}", on)
            for j in corners:
                nc.tensor.transpose(into[:, j, :], words[n, b][:, j // 2, :, j % 2].bitcast(F32), ident[:])
                turned[n, b, j] = into[:, j, :]

        def turn_both(s, b, h, on):
            into = bank(f"turned_both{s}_{b}_{h}", on)
            for u in range(2):
                for i in range(2):
                    nc.tensor.transpose(into[:, 2 * i + u, :], words[2 * s + u, b][:, h, :, i].bitcast(F32), ident[:])
            return into

        def corner(n, b, j):
            halves = turned[n, b, j].bitcast(BF16).rearrange("g (p e) -> g e p", e=2)
            return halves, weights[:, b, j : j + 1]

        def add_up(n, b, terms):
            s, u = pairs[n]
            for e in range(2):
                for i, term in enumerate(terms):
                    nc.tensor.matmul(
                        sums[s, b][:, 2 * u + e, :], term[:, e, :], ident[:],
                        start=(i == 0), stop=(i == len(terms) - 1), is_transpose=True,
                    )

        def add_up_by_terms(n, b, terms):
            s, u = pairs[n]
            for i, term in enumerate(terms):
                for e in range(2):
                    nc.tensor.matmul(
                        sums[s, b][:, 2 * u + e, :], term[:, e, :], ident[:],
                        start=(i == 0 and e == 0), stop=(i == len(terms) - 1 and e == 1), is_transpose=True,
                    )

        def weigh(n, b, corners, engine, on=None):
            weighted = sbuf([P, len(corners), 2, P], F32, f"weighted{n}_{b}_{corners[0]}", on)
            for i, j in enumerate(corners):
                halves, weight = corner(n, b, j)
                if engine == "scalar":
                    nc.scalar.activation(out=weighted[:, i], in_=halves, func=COPY, scale=weight)
                else:
                    nc.vector.tensor_scalar(out=weighted[:, i], in0=halves, scalar1=weight, scalar2=None, op0=MULT)
            return [weighted[:, i] for i in range(len(corners))]

        def weigh_onto(n, b, corners, terms, on=None):
            twos = sbuf([P, len(corners), 2, P], F32, f"twos{n}_{b}_{corners[0]}", on)
            for i, j in enumerate(corners):
                halves, weight = corner(n, b, j)
                nc.vector.scalar_tensor_tensor(
                    out=twos[:, i], in0=halves, scalar=weight, in1=terms[i], op0=MULT, op1=ADD
                )
            return [twos[:, i] for i in range(len(corners))]

        def weigh_both(s, b, both, on=None):
            weighted = sbuf([P, K, 2, 2, P], F32, f"weighted_both{s}_{b}", on)
            for j in range(K):
                halves = both[j // 2][:, 2 * (j % 2) : 2 * (j % 2) + 2, :].bitcast(BF16).rearrange("g u (p e) -> g u e p", e=2)
                nc.scalar.activation(out=weighted[:, j], in_=halves, func=COPY, scale=weights[:, b, j : j + 1])
            return [[weighted[:, j, u] for j in range(K)] for u in range(2)]

        def spread_weights(b, on, place):
            into = bank(f"spread_bank{b}", on)
            for j in range(K):
                nc.tensor.transpose(into[:, j, :], early_weights[:, j : j + 1].to_broadcast([P, P]), ident[:])
            spread = sbuf([P, 2, P, 2], F32, f"spread{b}", place)
            nc.scalar.copy(out=spread[:], in_=into[:].rearrange("p (h j) g -> p h g j", h=2))
            return spread

        def weigh_unturned(n, b, spread, on=None):
            weighted = sbuf([P, 2, ENTRIES], F32, f"unturned{n}_{b}", on)
            halves = words[n, b][:].rearrange("p h g j -> p (h g j)").bitcast(BF16).rearrange("p (c e) -> p e c", e=2)
            nc.gpsimd.tensor_tensor(
                out=weighted[:], in0=halves,
                in1=spread[:].rearrange("p h g j -> p (h g j)").unsqueeze(1).to_broadcast([P, 2, ENTRIES]), op=MULT,
            )
            return weighted[:].rearrange("p e (h g j) -> p e h g j", h=2, j=2)

        def sum_unturned(n, b, weighted):
            s, u = pairs[n]
            twos = sbuf([P, 2, P, 2], F32, f"unturned_twos{n}_{b}")
            nc.gpsimd.tensor_tensor(out=twos[:], in0=weighted[:, :, 0], in1=weighted[:, :, 1], op=ADD)
            nc.gpsimd.tensor_tensor(
                out=e_values[s, b][:, :, 2 * u : 2 * u + 2],
                in0=twos[:, :, :, 0].rearrange("p e g -> p g e"), in1=twos[:, :, :, 1].rearrange("p e g -> p g e"), op=ADD,
            )

        def add_halves(n, weighted, twos):
            u = n % 2
            nc.gpsimd.tensor_tensor(
                out=twos[:, :, 2 * u : 2 * u + 2, :],
                in0=weighted[:, :, 0].rearrange("p e g j -> p g e j"),
                in1=weighted[:, :, 1].rearrange("p e g j -> p g e j"),
                op=ADD,
            )

        def add_turning(n, weighted, into):
            u = n % 2
            for e in range(2):
                for j in range(K):
                    nc.tensor.matmul(
                        into[:, 2 * u + e, :], weighted[:, e, j // 2, :, j % 2], ident[:],
                        start=(j == 0), stop=(j == K - 1), is_transpose=True,
                    )

        def round_by_points(into, u, on):
            rounded = sbuf([P, P, 2], BF16, f"rounded{u}", on)
            nc.scalar.activation(
                out=rounded[:], in_=into[:, 2 * u : 2 * u + 2, :].rearrange("g e p -> g p e"), func=COPY
            )
            return rounded

        def turn_back(rounded, on):
            back = bank("back", on)
            for u in range(2):
                nc.tensor.transpose(back[:, u, :], rounded[u][:].rearrange("g p e -> g (p e)").bitcast(F32), ident[:])
            return back

        def copy_back(s, b, back):
            nc.scalar.copy(
                out=e_values[s, b][:].rearrange("p g t -> p (g t)").bitcast(F32).rearrange("p (g u) -> p g u", u=2),
                in_=back[:, 0:2, :].rearrange("p u g -> p g u"),
            )

        def round_e(s, b, engine="scalar", places=slice(0, PACK)):
            src = sums[s, b][:, places, :].rearrange("p t g -> p g t")
            if engine == "scalar":
                nc.scalar.activation(out=e_values[s, b][:, :, places], in_=src, func=COPY)
            else:
                nc.vector.tensor_copy(out=e_values[s, b][:, :, places], in_=src)

        def quantize_e(s, b, on=None):
            e_scales[s, b] = sbuf([P, P], U8, f"e_scales{s}_{b}", on)
            nc.vector.quantize_mx(
                out=e_codes[s][:, b * P : (b + 1) * P].bitcast(FP8X4),
                scales=e_scales[s, b][:],
                in_=e_values[s, b][:].rearrange("p g t -> p (g t)"),
            )

        def round_w():
            w_values = sbuf([P, PASSES, M, PACK], BF16, "w_values")
            nc.gpsimd.tensor_scalar(
                out=w_values[:], in0=w_whole[:].rearrange("p s t m -> p s m t"), scalar1=1.0, scalar2=0.0, op0=MULT, op1=ADD
            )
            return w_values

        def quantize_w(w_values, on):
            scales = sbuf([P, PASSES * M], U8, "w_scales", on)
            for s in range(PASSES):
                w_scales[s] = scales[:, s * M : (s + 1) * M]
            nc.vector.quantize_mx(
                out=w_codes[:].bitcast(FP8X4), scales=scales[:], in_=w_values[:].rearrange("p s m t -> p (s m t)")
            )

        def multiply(s, b):
            points = slice(b * P, (b + 1) * P)
            for i in range(CHANNELS):
                channels = slice(s * M + i * P, s * M + (i + 1) * P)
                nc.tensor.matmul_mx(
                    out=products[b, i][:, 0, :],
                    lhsT=w_codes[:, channels].bitcast(FP8X4),
                    lhsT_scale=w_scales[s][:, i * P : (i + 1) * P],
                    rhs=e_codes[s][:, points].bitcast(FP8X4),
                    rhs_scale=e_scales[s, b][:],
                    start=(s == 0),
                    stop=(s == PASSES - 1),
                )

        def finish(b, on=None):
            points = slice(b * P, (b + 1) * P)
            result = sbuf([P, CHANNELS, P], F32, f"result{b}", on)
            nc.vector.tensor_scalar(
                out=result[:, 0], in0=products[b, 0][:, 0, :], scalar1=bias_cols[:, 0:1], scalar2=None, op0=ADD
            )
            nc.scalar.activation(out=result[:, 1], in_=products[b, 1][:, 0, :], func=IDENTITY, bias=bias_cols[:, 1:2])
            if b == 0:
                nc.sync.dma_start(out=out_view[:, :, points], in_=result[:])
            else:
                nc.sync.dma_start(out=out_view[:, 0, points], in_=result[:, 0])
                nc.scalar.dma_start(out=out_view[:, 1, points], in_=result[:, 1])

        spread = spread_weights(0, "sums1_1", None)
        for s, b in ((0, 1), (1, 0), (1, 1)):
            sums[s, b] = bank(f"sums{s}_{b}", f"sums{s}_{b}")
        twos = sbuf([P, P, PACK, 2], F32, "unturned_twos")
        for h in range(2):
            cast(0, h, "vector")
        gather(0, 0)
        gather(0, 1)
        for n in range(1, 4):
            cast_low(n, 0)
            cast_low(n, 1)
            gather(n, 0)
            gather(n, 1)
        for n in range(2):
            add_halves(n, weigh_unturned(n, 0, spread), twos)
        w_values = round_w()
        both = [turn_both(0, 1, h, on) for h, on in enumerate(("a", "b"))]
        turn(2, 0, "c")
        turn(2, 1, "d")
        terms = weigh_both(0, 1, both, 512)
        turn(3, 0, "a")
        turn(3, 1, "b")
        add_up_by_terms(0, 1, terms[0])
        add_up_by_terms(1, 1, terms[1])
        even_20 = weigh(2, 0, (0, 2), "scalar", 8704)
        even_21 = weigh(2, 1, (0, 2), "scalar", 10752)
        even_30 = weigh(3, 0, (0, 2), "scalar", 16384)
        terms = weigh(3, 1, range(K), "scalar")
        add_up_by_terms(2, 0, weigh_onto(2, 0, (1, 3), even_20))
        add_up_by_terms(2, 1, weigh_onto(2, 1, (1, 3), even_21))
        add_up_by_terms(3, 0, weigh_onto(3, 0, (1, 3), even_30))
        add_up_by_terms(3, 1, terms)
        e_values[0, 0] = sbuf([P, P, PACK], BF16, "e_values0_0", 16384)
        nc.vector.tensor_tensor(out=e_values[0, 0][:], in0=twos[:, :, :, 0], in1=twos[:, :, :, 1], op=ADD)
        e_values[0, 1] = sbuf([P, P, PACK], BF16, "e_values0_1", "words3_1")
        e_values[1, 0] = sbuf([P, P, PACK], BF16, "e_values1_0")
        e_values[1, 1] = sbuf([P, P, PACK], BF16, "e_values1_1")
        round_e(0, 1)
        round_e(1, 0)
        round_e(1, 1)
        quantize_w(w_values, 17408)
        quantize_e(0, 0)
        quantize_e(0, 1)
        quantize_e(1, 0)
        quantize_e(1, 1)
        for (b, i), on in {(0, 0): "e", (0, 1): "c", (1, 0): "sums0_1", (1, 1): "d"}.items():
            products[b, i] = bank(f"products{b}_{i}", on)
        for s, b in ((0, 0), (0, 1), (1, 0), (1, 1)):
            multiply(s, b)
        finish(0, "e_values1_1")
        finish(1)
